import numpy as np
import ml_dtypes


def mxq(x, axis, fmt="e4m3"):
    dtype, down = {"e4m3": (ml_dtypes.float8_e4m3fn, 7), "e5m2": (ml_dtypes.float8_e5m2, 14)}[fmt]
    v = np.moveaxis(np.asarray(x, np.float32).astype(ml_dtypes.bfloat16).astype(np.float64), axis, -1)
    blocks = v.reshape(v.shape[:-1] + (-1, 32))
    amax = np.abs(blocks).max(-1, keepdims=True)
    byte = np.maximum(np.where(amax > 0, np.frexp(amax)[1] - 1 + 127, 0) - down, 1)
    scale = np.exp2(byte - 127.0)
    codes = (blocks / scale).astype(np.float32).astype(dtype).astype(np.float64)
    return np.moveaxis((codes * scale).reshape(v.shape), -1, axis)


WIDE = False


def mx_kscale(k):
    if not WIDE:
        return np.ones(k)
    levels = np.array([10, -10, 5, -5, 0])
    if k % 512:
        return np.exp2(np.random.permutation(np.resize(levels, k // 32))).repeat(32)
    a = np.empty((k // 512, 16))
    for p in range(k // 512):
        a[p, :8] = np.random.permutation(np.resize(levels, 8))
        for g in range(8):
            far = levels[np.abs(levels - a[p, g]) >= 10]
            a[p, g + 8] = far[np.random.randint(len(far))]
    return np.exp2(a.ravel()).repeat(32)


def f64(x):
    return np.asarray(x).astype(np.float64)


def striped(idx):
    return np.tile(np.asarray(idx).reshape(-1, 16).T, (8, 1)).astype(np.uint16)


def unstriped(offs):
    return offs[:16].T.reshape(-1).astype(np.int64)


def bf(x):
    return np.asarray(x, np.float32).astype(ml_dtypes.bfloat16)


def planes(Y):
    r, m = Y.shape
    b = f64(bf(Y)).reshape(r // 32, 32, m)
    amax = np.abs(b).max(1)
    byte = np.clip(np.where(amax > 0, np.frexp(amax)[1] - 1 + 127 - 7, 1), 1, 254)
    codes = (b * np.exp2(127.0 - byte)[:, None, :]).reshape(r, m).astype(np.float32).astype(ml_dtypes.float8_e4m3fn).view(np.uint8)
    words = codes.reshape(r // 512, 128, 4, m).transpose(0, 1, 3, 2)
    return np.ascontiguousarray(words), np.ascontiguousarray(byte.astype(np.uint8).reshape(r // 512, 16, m))


D, T, I, M = 512, 2048, 512, 512


def setup_inputs():
    n = np.random.standard_normal
    idx = np.random.permutation(T)[:I]
    fd = mx_kscale(D)
    fi = mx_kscale(I)
    return {
        "keys": (n((D, T)) / fd[:, None]).astype(np.float32),
        "cent": (n((D, M)) * 0.7 / np.sqrt(D) * fd[:, None]).astype(np.float32),
        "fac": (np.random.uniform(8.0, 32.0, (I, 1)) * fi[:, None]).astype(np.float32),
        "ksc": (np.random.uniform(0.5, 2.0, (I, 1)) / fi[:, None]).astype(np.float32),
        "dsc": (np.random.uniform(0.5, 2.0, (1, D)) * fd).astype(np.float32),
        "offs": striped(idx),
    }


def reference(keys, cent, fac, ksc, dsc, offs):
    idx = unstriped(offs)
    keysidxq = mxq(f64(keys)[:, idx], 0, "e4m3")
    centq = mxq(f64(cent), 0, "e4m3")
    a = keysidxq.T @ centq
    p = np.exp(a - np.max(a, axis=1, keepdims=True))
    w = p * f64(fac) / np.sum(p, axis=1, keepdims=True)
    kt = f64(keys)[:, idx].T
    ks = kt * f64(ksc) * f64(dsc)
    ksq = mxq(ks, 0, "e4m3")
    wq = mxq(w, 0, "e4m3")
    y = ksq.T @ wq
    words, scales = planes(y)
    return y, words, scales

@@ -1,0 +1,269 @@
+from contextlib import ExitStack
+
+import concourse.mybir as mybir
+from concourse.masks import make_identity
+
+D, T, I, M = 512, 2048, 512, 512
+FLOPS = 2 * 2 * D * I * M
+
+F32 = mybir.dt.float32
+BF16 = mybir.dt.bfloat16
+I32 = mybir.dt.int32
+U32 = mybir.dt.uint32
+U16 = mybir.dt.uint16
+U8 = mybir.dt.uint8
+FP8X4 = mybir.dt.float8_e4m3fn_x4
+MULT = mybir.AluOpType.mult
+MAX = mybir.AluOpType.max
+COPY = mybir.ActivationFunctionType.Copy
+EXP = mybir.ActivationFunctionType.Exp
+AXIS_X = mybir.AxisListType.X
+
+P = 128
+PACK = 4
+PART = 128
+
+
+def tile_attend_softcluster_pl_kernel(tc, keys, cent, fac, ksc, dsc, offs, out_0, out_1, out_2):
+    nc = tc.nc
+    with ExitStack() as ctx:
+        keep = ctx.enter_context(tc.tile_pool(name="keep", bufs=1))
+        psum = ctx.enter_context(tc.psum_pool(name="psum", bufs=1))
+
+        def sb(name, shape, dtype, tag=None):
+            return keep.tile(shape, dtype, name=name, tag=tag or name, align_bytes=64)
+
+        offsets = keep.tile([P, I // 16], U16, name="offsets")
+        cent_rows = cent.rearrange("(p t) m -> p t m", t=PACK)
+        early = M - PART
+        cent_early = sb("cent_early", [P, PACK, early], F32)
+        cent_late = sb("cent_late", [P, PACK, PART], F32)
+        nc.sync.dma_start(cent_early[:], cent_rows[:, :, :early])
+        nc.sync.dma_start(offsets[:], offs)
+        key_rows = keys.rearrange("(p t) n -> p t n", t=PACK)
+        pool = [sb("pool%d" % t, [P, T], F32) for t in range(PACK - 1)]
+        for t in range(PACK - 1):
+            nc.sync.dma_start(pool[t][:], key_rows[:, t, :])
+        ksc4 = sb("ksc4", [P, PACK], F32)
+        dsc4 = sb("dsc4", [P, PACK], F32)
+        fac4 = sb("fac4", [P, PACK], F32)
+        nc.scalar.dma_start(ksc4[:], ksc.rearrange("(s r) o -> s (r o)", r=PACK))
+        nc.scalar.dma_start(dsc4[:], dsc.rearrange("o (p t) -> p (o t)", t=PACK))
+        nc.scalar.dma_start(fac4[:], fac.rearrange("(s r) o -> s (r o)", r=PACK))
+
+        identity = sb("identity", [P, P], F32)
+        make_identity(nc, identity[:])
+        ksc_rows = psum.tile([P, PACK, P], F32, name="ksc_rows")
+        for r in range(PACK):
+            nc.tensor.transpose(ksc_rows[:, r, :], ksc4[:, r : r + 1].to_broadcast([P, P]), identity[:])
+
+        cent_codes = sb("cent_codes", [P, M + P], U32)
+        cent_scales = sb("cent_scales", [P, M + P], U8)
+        for lo, hi in ((0, 2 * PART), (2 * PART, early)):
+            cent_bf = sb("cent_bf%d" % lo, [P, (hi - lo) * PACK], BF16)
+            dst = cent_bf[:].rearrange("p (c i t) -> p c t i", i=4, t=PACK)
+            src = cent_early[:, :, lo:hi].rearrange("p t (c i) -> p c t i", i=4)
+            if lo == 0:
+                nc.vector.tensor_copy(dst, src)
+            else:
+                nc.scalar.activation(dst, src, COPY)
+            nc.vector.quantize_mx(cent_codes[:, lo:hi].bitcast(FP8X4), cent_scales[:, lo:hi], cent_bf[:])
+
+        picked = [sb("picked%d" % h, [P, 2, I], F32) for h in range(2)]
+        late_bf = sb("late_bf", [P, (PART + P) * PACK], BF16)
+        odd_bf = sb("odd_bf", [P, 2 * P * PACK], BF16)
+        even_bf = sb("even_bf", [P, P * PACK], BF16)
+        key_bf = [late_bf[:, PART * PACK :], odd_bf[:, : P * PACK], even_bf[:], odd_bf[:, P * PACK :]]
+        ks_codes = sb("ks_codes", [P, D], U32)
+        ks_scales = sb("ks_scales", [P, D], U8)
+        ks_bf = [sb("ks_bf%d" % h, [P, 2 * P * 2], F32) for h in range(2)]
+
+        def gather(t):
+            nc.vector.tensor_copy(picked[t // 2][:, t % 2, :], pool[t][:].indirect(offsets[:]))
+
+        def scale_keys(t, tag, factor):
+            ks_cols = sb("ks_cols%d" % t, [P, I], BF16, tag)
+            nc.vector.scalar_tensor_tensor(
+                ks_cols[:].rearrange("p (s r) -> p s r", r=PACK),
+                picked[t // 2][:, t % 2, :].rearrange("p (s r) -> p s r", r=PACK),
+                factor,
+                ksc_rows[:].rearrange("p r s -> p s r"),
+                MULT,
+                MULT,
+            )
+            return ks_cols
+
+        def turn_keys(t, ks_cols, bank, bufs):
+            turned = psum.tile([P, 2, P], F32, name="turned", tag=bank, bufs=bufs)
+            words = ks_cols[:].bitcast(F32)
+            for u in range(2):
+                nc.tensor.transpose(turned[:, u, :], words[:, u::2], identity[:])
+            half = ks_bf[t // 2][:, (t % 2) * 2 * P : (t % 2 + 1) * 2 * P]
+            nc.scalar.copy(half.rearrange("s (p u) -> s p u", u=2), turned[:].rearrange("s u p -> s p u"))
+
+        def quantise_ks(h):
+            cols = slice(h * 2 * P, (h + 1) * 2 * P)
+            nc.vector.quantize_mx(ks_codes[:, cols].bitcast(FP8X4), ks_scales[:, cols], ks_bf[h][:].bitcast(BF16))
+
+        def deal(h, r):
+            return (
+                key_bf[r].rearrange("p (s t) -> p s t", t=PACK)[:, :, 2 * h : 2 * h + 2],
+                picked[h][:].rearrange("p e (s r) -> p r s e", r=PACK)[:, r],
+            )
+
+        parked = [picked[0][:, 1, 0:1], picked[1][:, 0, 0:1]]
+        for t in range(2):
+            nc.vector.tensor_copy(parked[t], dsc4[:, t : t + 1])
+        gather(0)
+        pool.append(sb("pool3", [P, T], F32, "pool0"))
+        nc.sync.dma_start(pool[3][:], key_rows[:, 3, :])
+        nc.sync.dma_start(cent_late[:], cent_rows[:, :, early:])
+        turn_keys(0, scale_keys(0, "ks_cols0", parked[0]), "turned", 2)
+        gather(1)
+        for r in range(PACK):
+            dst, src = deal(0, r)
+            nc.scalar.activation(dst, src, COPY)
+        turn_keys(1, scale_keys(1, "ks_cols1", parked[1]), "turned", 2)
+        gather(2)
+        turn_keys(2, scale_keys(2, "ks_cols2", dsc4[:, 2:3]), "turned", 2)
+        quantise_ks(0)
+        gather(3)
+
+        odd_codes = sb("odd_codes", [P, 2 * P], U32)
+        odd_scales = sb("odd_scales", [P, 2 * P], U8)
+        even_codes = sb("even_codes", [P, P], U32)
+        even_scales = sb("even_scales", [P, P], U8)
+        key_codes = [cent_codes[:, M:], odd_codes[:, :P], even_codes[:], odd_codes[:, P:]]
+        key_scales = [cent_scales[:, M:], odd_scales[:, :P], even_scales[:], odd_scales[:, P:]]
+        scores = [psum.tile([P, M], F32, name="bank%d" % r) for r in range(PACK)]
+        neg_max = [sb("neg_max%d" % r, [P, 1], F32) for r in range(PACK)]
+        total = sb("total", [P, PACK], F32)
+        inverse = sb("inverse", [P, PACK], F32)
+        expd = [sb("expd%d" % r, [P, M], F32) for r in range(PACK)]
+        w_rows = sb("w_rows", [P, PACK, M], BF16)
+
+        def score(r):
+            nc.tensor.matmul_mx(
+                scores[r][:],
+                lhsT=key_codes[r].bitcast(FP8X4),
+                lhsT_scale=key_scales[r],
+                rhs=cent_codes[:, :M].bitcast(FP8X4),
+                rhs_scale=cent_scales[:, :M],
+                start=True,
+                stop=True,
+            )
+
+        def soft(r):
+            nc.vector.tensor_reduce(neg_max[r][:], scores[r][:], AXIS_X, MAX, negate=True)
+            nc.scalar.activation(expd[r][:], scores[r][:], EXP, bias=neg_max[r][:], accum_out=total[:, r : r + 1])
+
+        nc.vector.tensor_copy(
+            late_bf[:, : PART * PACK].rearrange("p (c i t) -> p c t i", i=4, t=PACK),
+            cent_late[:].rearrange("p t (c i) -> p c t i", i=4),
+        )
+        for r in range(PACK):
+            dst, src = deal(1, r)
+            if r % 2:
+                nc.scalar.activation(dst, src, COPY)
+            else:
+                nc.vector.tensor_copy(dst, src)
+        nc.vector.quantize_mx(cent_codes[:, early:].bitcast(FP8X4), cent_scales[:, early:], late_bf[:])
+        score(0)
+        nc.vector.quantize_mx(even_codes[:].bitcast(FP8X4), even_scales[:], even_bf[:])
+        score(2)
+        ks_last = scale_keys(3, "even_bf", dsc4[:, 3:4])
+        nc.vector.quantize_mx(odd_codes[:].bitcast(FP8X4), odd_scales[:], odd_bf[:])
+        score(1)
+        score(3)
+        for r in (0, 2, 1, 3):
+            soft(r)
+
+        parts = M // PART
+        w_bf = [sb("w_bf%d" % q, [P, PART, PACK], BF16) for q in range(parts)]
+        w_codes = [sb("w_codes%d" % q, [P, PART], U32) for q in range(parts)]
+        w_scales = [sb("w_scales%d" % q, [P, PART], U8) for q in range(parts)]
+        y_rows = [sb("y_rows%d" % q, [P, PACK, PART], F32) for q in range(parts)]
+        y_bf = sb("y_bf", [P, M * PACK], BF16)
+        y_codes = sb("y_codes", [P, M], U32)
+        y_scales = sb("y_scales", [P, M], U8)
+        out_rows = out_0.rearrange("(p t) m -> p t m", t=PACK)
+
+        def invert(rows):
+            nc.vector.reciprocal(inverse[:, rows], total[:, rows])
+
+        def weigh(dst, r, cols):
+            nc.vector.tensor_scalar(dst, expd[r][:, cols], inverse[:, r : r + 1], fac4[:, r : r + 1], MULT, MULT)
+
+        def weave(q, rows, move):
+            cols = slice(q * PART, (q + 1) * PART)
+            move(
+                w_bf[q][:, :, :rows].rearrange("s (c i) r -> s c r i", i=4),
+                w_rows[:, :rows, cols].rearrange("s r (c i) -> s c r i", i=4),
+            )
+
+        def quantise_w(q):
+            nc.vector.quantize_mx(w_codes[q][:].bitcast(FP8X4), w_scales[q][:], w_bf[q][:].rearrange("s m r -> s (m r)"))
+
+        def product(q, planes, tag, bufs):
+            sums = psum.tile([P, len(planes), PART], F32, name="sums", tag=tag, bufs=bufs)
+            for t in planes:
+                nc.tensor.matmul_mx(
+                    sums[:, t - planes[0], :],
+                    lhsT=ks_codes[:, t * P : (t + 1) * P].bitcast(FP8X4),
+                    lhsT_scale=ks_scales[:, t * P : (t + 1) * P],
+                    rhs=w_codes[q][:].bitcast(FP8X4),
+                    rhs_scale=w_scales[q][:],
+                    start=True,
+                    stop=True,
+                )
+            return sums
+
+        def hand_on(q, src):
+            cols = slice(q * PART, (q + 1) * PART)
+            wide = slice(q * PART * PACK, (q + 1) * PART * PACK)
+            nc.vector.tensor_copy(
+                y_bf[:, wide].rearrange("p (c i t) -> p c t i", i=4, t=PACK),
+                src[:].rearrange("p t (c i) -> p c t i", i=4),
+            )
+            nc.vector.quantize_mx(y_codes[:, cols].bitcast(FP8X4), y_scales[:, cols], y_bf[:, wide])
+
+        last = PACK - 1
+        invert(slice(0, 3, 2))
+        weigh(w_rows[:, 0, :], 0, slice(0, M))
+        invert(slice(1, 2))
+        weigh(w_rows[:, 2, :], 2, slice(0, M))
+        weigh(w_rows[:, 1, :], 1, slice(0, M))
+        turn_keys(3, ks_last, "bank1", 1)
+        invert(slice(3, 4))
+        weave(0, last, nc.vector.tensor_copy)
+        weigh(w_bf[0][:, :, last], last, slice(0, PART))
+        weigh(w_rows[:, last, PART:], last, slice(PART, M))
+        quantise_w(0)
+        quantise_ks(1)
+        weave(1, PACK, nc.scalar.copy)
+        weave(2, PACK, nc.scalar.copy)
+        weave(3, PACK, nc.vector.tensor_copy)
+        banks = [product(0, range(PACK), "bank0", 1)]
+        for q, tag in ((1, "ksc_rows"), (2, "bank2")):
+            quantise_w(q)
+            banks.append(product(q, range(PACK), tag, 1))
+        quantise_w(3)
+        halves = [product(3, range(2), "bank3", 1), product(3, range(2, PACK), "turned", 2)]
+
+        for q in range(parts):
+            if q < parts - 1:
+                nc.scalar.copy(y_rows[q][:], banks[q][:])
+            else:
+                nc.scalar.copy(y_rows[q][:, :2, :], halves[0][:])
+                nc.vector.tensor_copy(y_rows[q][:, 2:, :], halves[1][:])
+            nc.sync.dma_start(out_rows[:, :, q * PART : (q + 1) * PART], y_rows[q][:])
+        for q in range(parts):
+            hand_on(q, y_rows[q])
+        out_words = out_1.rearrange("z p m t -> p (z m t)").bitcast(I32)
+        for cols in (slice(0, early), slice(early, M)):
+            nc.sync.dma_start(out_words[:, cols], y_codes[:, cols].bitcast(I32))
+        for quad in range(4):
+            queue = nc.scalar if quad % 2 else nc.sync
+            queue.dma_start(
+                out_2[0, 4 * quad : 4 * quad + 4, :].bitcast(I32), y_scales[32 * quad : 32 * quad + 4, :].bitcast(I32)
+            )

@@ -38,12 +38,13 @@ def tile_attend_softcluster_pl_kernel(tc, keys, cent, fac, ksc, dsc, offs, out_0
         early = M - PART
         cent_early = sb("cent_early", [P, PACK, early], F32)
         cent_late = sb("cent_late", [P, PACK, PART], F32)
-        nc.sync.dma_start(cent_early[:], cent_rows[:, :, :early])
-        nc.sync.dma_start(offsets[:], offs)
         key_rows = keys.rearrange("(p t) n -> p t n", t=PACK)
         pool = [sb("pool%d" % t, [P, T], F32) for t in range(PACK - 1)]
-        for t in range(PACK - 1):
-            nc.sync.dma_start(pool[t][:], key_rows[:, t, :])
+        nc.sync.dma_start(pool[0][:], key_rows[:, 0, :])
+        nc.sync.dma_start(offsets[:], offs)
+        nc.sync.dma_start(pool[1][:], key_rows[:, 1, :])
+        nc.sync.dma_start(cent_early[:], cent_rows[:, :, :early])
+        nc.sync.dma_start(pool[2][:], key_rows[:, 2, :])
         ksc4 = sb("ksc4", [P, PACK], F32)
         dsc4 = sb("dsc4", [P, PACK], F32)
         fac4 = sb("fac4", [P, PACK], F32)
@@ -59,22 +60,12 @@ def tile_attend_softcluster_pl_kernel(tc, keys, cent, fac, ksc, dsc, offs, out_0
 
         cent_codes = sb("cent_codes", [P, M + P], U32)
         cent_scales = sb("cent_scales", [P, M + P], U8)
-        for lo, hi in ((0, 2 * PART), (2 * PART, early)):
-            cent_bf = sb("cent_bf%d" % lo, [P, (hi - lo) * PACK], BF16)
-            dst = cent_bf[:].rearrange("p (c i t) -> p c t i", i=4, t=PACK)
-            src = cent_early[:, :, lo:hi].rearrange("p t (c i) -> p c t i", i=4)
-            if lo == 0:
-                nc.vector.tensor_copy(dst, src)
-            else:
-                nc.scalar.activation(dst, src, COPY)
-            nc.vector.quantize_mx(cent_codes[:, lo:hi].bitcast(FP8X4), cent_scales[:, lo:hi], cent_bf[:])
 
-        picked = [sb("picked%d" % h, [P, 2, I], F32) for h in range(2)]
+        picked = [sb("picked0", [P, 2, I], F32)]
         late_bf = sb("late_bf", [P, (PART + P) * PACK], BF16)
         odd_bf = sb("odd_bf", [P, 2 * P * PACK], BF16)
         even_bf = sb("even_bf", [P, P * PACK], BF16)
         key_bf = [late_bf[:, PART * PACK :], odd_bf[:, : P * PACK], even_bf[:], odd_bf[:, P * PACK :]]
-        ks_codes = sb("ks_codes", [P, D], U32)
         ks_scales = sb("ks_scales", [P, D], U8)
         ks_bf = [sb("ks_bf%d" % h, [P, 2 * P * 2], F32) for h in range(2)]
 
@@ -111,20 +102,32 @@ def tile_attend_softcluster_pl_kernel(tc, keys, cent, fac, ksc, dsc, offs, out_0
                 picked[h][:].rearrange("p e (s r) -> p r s e", r=PACK)[:, r],
             )
 
-        parked = [picked[0][:, 1, 0:1], picked[1][:, 0, 0:1]]
-        for t in range(2):
-            nc.vector.tensor_copy(parked[t], dsc4[:, t : t + 1])
+        parked = picked[0][:, 1, 0:1]
+        nc.scalar.activation(parked, dsc4[:, 0:1], COPY)
         gather(0)
         pool.append(sb("pool3", [P, T], F32, "pool0"))
         nc.sync.dma_start(pool[3][:], key_rows[:, 3, :])
         nc.sync.dma_start(cent_late[:], cent_rows[:, :, early:])
-        turn_keys(0, scale_keys(0, "ks_cols0", parked[0]), "turned", 2)
+        turn_keys(0, scale_keys(0, "ks_cols0", parked), "turned", 2)
         gather(1)
         for r in range(PACK):
             dst, src = deal(0, r)
             nc.scalar.activation(dst, src, COPY)
-        turn_keys(1, scale_keys(1, "ks_cols1", parked[1]), "turned", 2)
+        turn_keys(1, scale_keys(1, "ks_cols1", dsc4[:, 1:2]), "turned", 2)
+        cent_bf = sb("cent_bf", [P, early * PACK], BF16, "ks_cols0")
+        pieces = ((0, 2 * PART), (2 * PART, early))
+        for lo, hi in pieces:
+            nc.vector.tensor_copy(
+                cent_bf[:, lo * PACK : hi * PACK].rearrange("p (c i t) -> p c t i", i=4, t=PACK),
+                cent_early[:, :, lo:hi].rearrange("p t (c i) -> p c t i", i=4),
+            )
+        for lo, hi in pieces:
+            nc.vector.quantize_mx(
+                cent_codes[:, lo:hi].bitcast(FP8X4), cent_scales[:, lo:hi], cent_bf[:, lo * PACK : hi * PACK]
+            )
+        picked.append(sb("picked1", [P, 2, I], F32, "ks_cols0"))
         gather(2)
+        ks_codes = sb("ks_codes", [P, D], U32, "pool2")
         turn_keys(2, scale_keys(2, "ks_cols2", dsc4[:, 2:3]), "turned", 2)
         quantise_ks(0)
         gather(3)
@@ -240,9 +243,9 @@ def tile_attend_softcluster_pl_kernel(tc, keys, cent, fac, ksc, dsc, offs, out_0
         weigh(w_rows[:, last, PART:], last, slice(PART, M))
         quantise_w(0)
         quantise_ks(1)
-        weave(1, PACK, nc.scalar.copy)
         weave(2, PACK, nc.scalar.copy)
-        weave(3, PACK, nc.vector.tensor_copy)
+        weave(1, PACK, nc.vector.tensor_copy)
+        weave(3, PACK, nc.scalar.copy)
         banks = [product(0, range(PACK), "bank0", 1)]
         for q, tag in ((1, "ksc_rows"), (2, "bank2")):
             quantise_w(q)

@@ -237,6 +237,17 @@ def tile_attend_softcluster_pl_kernel(tc, keys, cent, fac, ksc, dsc, offs, out_0
         weigh(w_rows[:, 2, :], 2, slice(0, M))
         weigh(w_rows[:, 1, :], 1, slice(0, M))
         turn_keys(3, ks_last, "bank1", 1)
+        warm = psum.tile([P, M], F32, name="warm", tag="bank3")
+        for r in range(2):
+            nc.tensor.matmul_mx(
+                warm[:],
+                lhsT=key_codes[r].bitcast(FP8X4),
+                lhsT_scale=key_scales[r],
+                rhs=cent_codes[:, :M].bitcast(FP8X4),
+                rhs_scale=cent_scales[:, :M],
+                start=True,
+                stop=True,
+            )
         invert(slice(3, 4))
         weave(0, last, nc.vector.tensor_copy)
         weigh(w_bf[0][:, :, last], last, slice(0, PART))

@@ -22,6 +22,9 @@ AXIS_X = mybir.AxisListType.X
 P = 128
 PACK = 4
 PART = 128
+HALF = 256
+SHARES = (192, 128)
+LAST_SHARE = 48
 
 
 def tile_attend_softcluster_pl_kernel(tc, keys, cent, fac, ksc, dsc, offs, out_0, out_1, out_2):
@@ -33,18 +36,31 @@ def tile_attend_softcluster_pl_kernel(tc, keys, cent, fac, ksc, dsc, offs, out_0
         def sb(name, shape, dtype, tag=None):
             return keep.tile(shape, dtype, name=name, tag=tag or name, align_bytes=64)
 
+        def quantise(codes, scales, values):
+            nc.vector.quantize_mx(codes.bitcast(FP8X4), scales, values)
+
+        def multiply(out, lhs_codes, lhs_scales, rhs_codes, rhs_scales):
+            nc.tensor.matmul_mx(
+                out,
+                lhsT=lhs_codes.bitcast(FP8X4),
+                lhsT_scale=lhs_scales,
+                rhs=rhs_codes.bitcast(FP8X4),
+                rhs_scale=rhs_scales,
+                start=True,
+                stop=True,
+            )
+
+        def weave(move, dst, src):
+            move(dst.rearrange("p (c i t) -> p c t i", i=4, t=PACK), src.rearrange("p t (c i) -> p c t i", i=4))
+
         offsets = keep.tile([P, I // 16], U16, name="offsets")
         cent_rows = cent.rearrange("(p t) m -> p t m", t=PACK)
-        early = M - PART
-        cent_early = sb("cent_early", [P, PACK, early], F32)
-        cent_late = sb("cent_late", [P, PACK, PART], F32)
         key_rows = keys.rearrange("(p t) n -> p t n", t=PACK)
-        pool = [sb("pool%d" % t, [P, T], F32) for t in range(PACK - 1)]
+        pool = [sb("pool%d" % t, [P, T], F32) for t in range(PACK)]
         nc.sync.dma_start(pool[0][:], key_rows[:, 0, :])
         nc.sync.dma_start(offsets[:], offs)
-        nc.sync.dma_start(pool[1][:], key_rows[:, 1, :])
-        nc.sync.dma_start(cent_early[:], cent_rows[:, :, :early])
-        nc.sync.dma_start(pool[2][:], key_rows[:, 2, :])
+        for t in range(1, PACK):
+            nc.sync.dma_start(pool[t][:], key_rows[:, t, :])
         ksc4 = sb("ksc4", [P, PACK], F32)
         dsc4 = sb("dsc4", [P, PACK], F32)
         fac4 = sb("fac4", [P, PACK], F32)
@@ -58,226 +74,217 @@ def tile_attend_softcluster_pl_kernel(tc, keys, cent, fac, ksc, dsc, offs, out_0
         for r in range(PACK):
             nc.tensor.transpose(ksc_rows[:, r, :], ksc4[:, r : r + 1].to_broadcast([P, P]), identity[:])
 
-        cent_codes = sb("cent_codes", [P, M + P], U32)
-        cent_scales = sb("cent_scales", [P, M + P], U8)
+        picked = [sb("picked%d" % h, [P, 2, I], F32) for h in range(2)]
+        key_bf = sb("key_bf", [P, PACK * P * PACK], BF16)
+        ks_bf = sb("ks_bf", [P, PACK * 2 * P], F32)
+        ks_cols = [sb("ks_cols%d" % t, [P, I], BF16) for t in range(PACK - 1)]
+        nc.scalar.activation(picked[0][:, 1, ::HALF], dsc4[:, 0:1].to_broadcast([P, 2]), COPY)
+        nc.scalar.activation(picked[1][:, :, ::HALF], dsc4[:, 1:3].unsqueeze(2).to_broadcast([P, 2, 2]), COPY)
 
-        picked = [sb("picked0", [P, 2, I], F32)]
-        late_bf = sb("late_bf", [P, (PART + P) * PACK], BF16)
-        odd_bf = sb("odd_bf", [P, 2 * P * PACK], BF16)
-        even_bf = sb("even_bf", [P, P * PACK], BF16)
-        key_bf = [late_bf[:, PART * PACK :], odd_bf[:, : P * PACK], even_bf[:], odd_bf[:, P * PACK :]]
-        ks_scales = sb("ks_scales", [P, D], U8)
-        ks_bf = [sb("ks_bf%d" % h, [P, 2 * P * 2], F32) for h in range(2)]
+        def factor(t, lo):
+            if t == PACK - 1:
+                return dsc4[:, t : t + 1]
+            return picked[(t + 1) // 2][:, (t + 1) % 2, lo : lo + 1]
 
-        def gather(t):
-            nc.vector.tensor_copy(picked[t // 2][:, t % 2, :], pool[t][:].indirect(offsets[:]))
+        def gather(t, lo, hi):
+            nc.vector.tensor_copy(picked[t // 2][:, t % 2, lo:hi], pool[t][:].indirect(offsets[:, lo // 16 : hi // 16]))
 
-        def scale_keys(t, tag, factor):
-            ks_cols = sb("ks_cols%d" % t, [P, I], BF16, tag)
+        def scale_keys(t, lo, hi):
             nc.vector.scalar_tensor_tensor(
-                ks_cols[:].rearrange("p (s r) -> p s r", r=PACK),
-                picked[t // 2][:, t % 2, :].rearrange("p (s r) -> p s r", r=PACK),
-                factor,
-                ksc_rows[:].rearrange("p r s -> p s r"),
+                ks_cols[t][:, lo:hi].rearrange("p (s r) -> p s r", r=PACK),
+                picked[t // 2][:, t % 2, lo:hi].rearrange("p (s r) -> p s r", r=PACK),
+                factor(t, lo),
+                ksc_rows[:, :, lo // PACK : hi // PACK].rearrange("p r s -> p s r"),
                 MULT,
                 MULT,
             )
-            return ks_cols
 
-        def turn_keys(t, ks_cols, bank, bufs):
-            turned = psum.tile([P, 2, P], F32, name="turned", tag=bank, bufs=bufs)
-            words = ks_cols[:].bitcast(F32)
+        def turn_keys(t):
+            turned = psum.tile([P, 2, P], F32, name="turned", tag="turned", bufs=2)
+            words = ks_cols[t][:].bitcast(F32)
             for u in range(2):
                 nc.tensor.transpose(turned[:, u, :], words[:, u::2], identity[:])
-            half = ks_bf[t // 2][:, (t % 2) * 2 * P : (t % 2 + 1) * 2 * P]
-            nc.scalar.copy(half.rearrange("s (p u) -> s p u", u=2), turned[:].rearrange("s u p -> s p u"))
+            plane = ks_bf[:, t * 2 * P : (t + 1) * 2 * P]
+            nc.scalar.copy(plane.rearrange("s (p u) -> s p u", u=2), turned[:].rearrange("s u p -> s p u"))
 
-        def quantise_ks(h):
-            cols = slice(h * 2 * P, (h + 1) * 2 * P)
-            nc.vector.quantize_mx(ks_codes[:, cols].bitcast(FP8X4), ks_scales[:, cols], ks_bf[h][:].bitcast(BF16))
-
-        def deal(h, r):
-            return (
-                key_bf[r].rearrange("p (s t) -> p s t", t=PACK)[:, :, 2 * h : 2 * h + 2],
-                picked[h][:].rearrange("p e (s r) -> p r s e", r=PACK)[:, r],
+        def deal(move, h, lo, hi):
+            move(
+                key_bf[:].rearrange("p (r s t) -> p s r t", r=PACK, t=PACK)[
+                    :, lo // PACK : hi // PACK, :, 2 * h : 2 * h + 2
+                ],
+                picked[h][:, :, lo:hi].rearrange("p e (s r) -> p s r e", r=PACK),
             )
 
-        parked = picked[0][:, 1, 0:1]
-        nc.scalar.activation(parked, dsc4[:, 0:1], COPY)
-        gather(0)
-        pool.append(sb("pool3", [P, T], F32, "pool0"))
-        nc.sync.dma_start(pool[3][:], key_rows[:, 3, :])
-        nc.sync.dma_start(cent_late[:], cent_rows[:, :, early:])
-        turn_keys(0, scale_keys(0, "ks_cols0", parked), "turned", 2)
-        gather(1)
-        for r in range(PACK):
-            dst, src = deal(0, r)
-            nc.scalar.activation(dst, src, COPY)
-        turn_keys(1, scale_keys(1, "ks_cols1", dsc4[:, 1:2]), "turned", 2)
-        cent_bf = sb("cent_bf", [P, early * PACK], BF16, "ks_cols0")
-        pieces = ((0, 2 * PART), (2 * PART, early))
-        for lo, hi in pieces:
-            nc.vector.tensor_copy(
-                cent_bf[:, lo * PACK : hi * PACK].rearrange("p (c i t) -> p c t i", i=4, t=PACK),
-                cent_early[:, :, lo:hi].rearrange("p t (c i) -> p c t i", i=4),
-            )
-        for lo, hi in pieces:
-            nc.vector.quantize_mx(
-                cent_codes[:, lo:hi].bitcast(FP8X4), cent_scales[:, lo:hi], cent_bf[:, lo * PACK : hi * PACK]
-            )
-        picked.append(sb("picked1", [P, 2, I], F32, "ks_cols0"))
-        gather(2)
-        ks_codes = sb("ks_codes", [P, D], U32, "pool2")
-        turn_keys(2, scale_keys(2, "ks_cols2", dsc4[:, 2:3]), "turned", 2)
-        quantise_ks(0)
-        gather(3)
+        ks_codes = sb("ks_codes", [P, D], U32)
+        ks_scales = sb("ks_scales", [P, D], U8)
 
-        odd_codes = sb("odd_codes", [P, 2 * P], U32)
-        odd_scales = sb("odd_scales", [P, 2 * P], U8)
-        even_codes = sb("even_codes", [P, P], U32)
-        even_scales = sb("even_scales", [P, P], U8)
-        key_codes = [cent_codes[:, M:], odd_codes[:, :P], even_codes[:], odd_codes[:, P:]]
-        key_scales = [cent_scales[:, M:], odd_scales[:, :P], even_scales[:], odd_scales[:, P:]]
+        def quantise_ks(lo, hi):
+            cols = slice(lo * P, hi * P)
+            quantise(ks_codes[:, cols], ks_scales[:, cols], ks_bf[:, lo * 2 * P : hi * 2 * P].bitcast(BF16))
+
+        for t in range(PACK - 1):
+            for lo in (0, HALF):
+                gather(t, lo, lo + HALF)
+            if t == 2:
+                quantise_ks(0, 2)
+            for lo in (0, HALF):
+                scale_keys(t, lo, lo + HALF)
+            turn_keys(t)
+            if t == 1:
+                deal(nc.scalar.copy, 0, 0, I)
+        cent_raw = []
+        for h in range(2):
+            cent_raw.append(sb("cent_raw%d" % h, [P, PACK, HALF], F32))
+            nc.sync.dma_start(cent_raw[h][:], cent_rows[:, :, h * HALF : (h + 1) * HALF])
+
+        key_codes = sb("key_codes", [P, PACK * P], U32)
+        key_scales = sb("key_scales", [P, PACK * P], U8)
+        cent_bf = []
+        cent_codes = sb("cent_codes", [P, M], U32)
+        cent_scales = sb("cent_scales", [P, M], U8)
+        last = PACK - 1
+        gather(last, 0, HALF)
+        gather(last, HALF, I)
+        deal(nc.scalar.copy, 1, 0, HALF)
+        quantise_ks(2, 3)
+        deal(nc.vector.tensor_copy, 1, HALF, I)
+
+        def weave_cent(h, tag):
+            cut = SHARES[h]
+            cent_bf.append(sb("cent_bf%d" % h, [P, HALF * PACK], BF16, tag))
+            weave(nc.vector.tensor_copy, cent_bf[h][:, cut * PACK :], cent_raw[h][:, :, cut:])
+            weave(nc.scalar.copy, cent_bf[h][:, : cut * PACK], cent_raw[h][:, :, :cut])
+
+        weave_cent(0, "pool3")
+        quantise(key_codes[:], key_scales[:], key_bf[:])
+        weave_cent(1, "cent_raw0")
+        for h in range(2):
+            cols = slice(h * HALF, (h + 1) * HALF)
+            quantise(cent_codes[:, cols], cent_scales[:, cols], cent_bf[h][:])
+        ks_cols.append(sb("ks_cols3", [P, I], BF16, "cent_raw0"))
+        scale_keys(last, 0, I)
+
         scores = [psum.tile([P, M], F32, name="bank%d" % r) for r in range(PACK)]
         neg_max = [sb("neg_max%d" % r, [P, 1], F32) for r in range(PACK)]
         total = sb("total", [P, PACK], F32)
         inverse = sb("inverse", [P, PACK], F32)
         expd = [sb("expd%d" % r, [P, M], F32) for r in range(PACK)]
+        share = sb("share", [P, PACK], F32)
         w_rows = sb("w_rows", [P, PACK, M], BF16)
 
-        def score(r):
-            nc.tensor.matmul_mx(
-                scores[r][:],
-                lhsT=key_codes[r].bitcast(FP8X4),
-                lhsT_scale=key_scales[r],
-                rhs=cent_codes[:, :M].bitcast(FP8X4),
-                rhs_scale=cent_scales[:, :M],
-                start=True,
-                stop=True,
-            )
+        def score(r, cols):
+            slots = slice(r * P, (r + 1) * P)
+            multiply(scores[r][:, cols], key_codes[:, slots], key_scales[:, slots], cent_codes[:, cols], cent_scales[:, cols])
 
-        def soft(r):
+        score(0, slice(0, HALF))
+        score(0, slice(HALF, M))
+        for r in range(1, PACK):
+            score(r, slice(0, M))
+
+        def invert(lo, hi):
+            nc.vector.reciprocal(inverse[:, lo:hi], total[:, lo:hi])
+
+        for r in range(PACK):
+            if r == last:
+                invert(0, 1)
             nc.vector.tensor_reduce(neg_max[r][:], scores[r][:], AXIS_X, MAX, negate=True)
             nc.scalar.activation(expd[r][:], scores[r][:], EXP, bias=neg_max[r][:], accum_out=total[:, r : r + 1])
-
-        nc.vector.tensor_copy(
-            late_bf[:, : PART * PACK].rearrange("p (c i t) -> p c t i", i=4, t=PACK),
-            cent_late[:].rearrange("p t (c i) -> p c t i", i=4),
-        )
-        for r in range(PACK):
-            dst, src = deal(1, r)
-            if r % 2:
-                nc.scalar.activation(dst, src, COPY)
-            else:
-                nc.vector.tensor_copy(dst, src)
-        nc.vector.quantize_mx(cent_codes[:, early:].bitcast(FP8X4), cent_scales[:, early:], late_bf[:])
-        score(0)
-        nc.vector.quantize_mx(even_codes[:].bitcast(FP8X4), even_scales[:], even_bf[:])
-        score(2)
-        ks_last = scale_keys(3, "even_bf", dsc4[:, 3:4])
-        nc.vector.quantize_mx(odd_codes[:].bitcast(FP8X4), odd_scales[:], odd_bf[:])
-        score(1)
-        score(3)
-        for r in (0, 2, 1, 3):
-            soft(r)
-
+        turn_keys(last)
+        warm = psum.tile([P, M], F32, name="warm", tag="bank3")
+        for r in range(2):
+            slots = slice(r * P, (r + 1) * P)
+            multiply(warm[:], key_codes[:, slots], key_scales[:, slots], cent_codes[:], cent_scales[:])
         parts = M // PART
-        w_bf = [sb("w_bf%d" % q, [P, PART, PACK], BF16) for q in range(parts)]
+        w_bf = [sb("w_bf%d" % q, [P, PART * PACK], BF16)[:] for q in range(parts)]
         w_codes = [sb("w_codes%d" % q, [P, PART], U32) for q in range(parts)]
         w_scales = [sb("w_scales%d" % q, [P, PART], U8) for q in range(parts)]
         y_rows = [sb("y_rows%d" % q, [P, PACK, PART], F32) for q in range(parts)]
-        y_bf = sb("y_bf", [P, M * PACK], BF16)
+        y_bf = [sb("y_bf%d" % q, [P, PART * PACK], BF16) for q in range(parts)]
         y_codes = sb("y_codes", [P, M], U32)
         y_scales = sb("y_scales", [P, M], U8)
         out_rows = out_0.rearrange("(p t) m -> p t m", t=PACK)
 
-        def invert(rows):
-            nc.vector.reciprocal(inverse[:, rows], total[:, rows])
-
         def weigh(dst, r, cols):
             nc.vector.tensor_scalar(dst, expd[r][:, cols], inverse[:, r : r + 1], fac4[:, r : r + 1], MULT, MULT)
 
-        def weave(q, rows, move):
-            cols = slice(q * PART, (q + 1) * PART)
-            move(
-                w_bf[q][:, :, :rows].rearrange("s (c i) r -> s c r i", i=4),
-                w_rows[:, :rows, cols].rearrange("s r (c i) -> s c r i", i=4),
-            )
+        def weave_w(move, q):
+            weave(move, w_bf[q], w_rows[:, :, q * PART : (q + 1) * PART])
 
         def quantise_w(q):
-            nc.vector.quantize_mx(w_codes[q][:].bitcast(FP8X4), w_scales[q][:], w_bf[q][:].rearrange("s m r -> s (m r)"))
+            quantise(w_codes[q][:], w_scales[q][:], w_bf[q])
 
         def product(q, planes, tag, bufs):
             sums = psum.tile([P, len(planes), PART], F32, name="sums", tag=tag, bufs=bufs)
             for t in planes:
-                nc.tensor.matmul_mx(
-                    sums[:, t - planes[0], :],
-                    lhsT=ks_codes[:, t * P : (t + 1) * P].bitcast(FP8X4),
-                    lhsT_scale=ks_scales[:, t * P : (t + 1) * P],
-                    rhs=w_codes[q][:].bitcast(FP8X4),
-                    rhs_scale=w_scales[q][:],
-                    start=True,
-                    stop=True,
-                )
+                rows = slice(t * P, (t + 1) * P)
+                multiply(sums[:, t - planes[0], :], ks_codes[:, rows], ks_scales[:, rows], w_codes[q][:], w_scales[q][:])
             return sums
 
-        def hand_on(q, src):
+        def weave_y(q):
+            cut = LAST_SHARE if q == parts - 1 else 0
+            weave(nc.vector.tensor_copy, y_bf[q][:, cut * PACK :], y_rows[q][:, :, cut:])
+            if cut:
+                weave(nc.scalar.copy, y_bf[q][:, : cut * PACK], y_rows[q][:, :, :cut])
+
+        def quantise_y(q):
             cols = slice(q * PART, (q + 1) * PART)
-            wide = slice(q * PART * PACK, (q + 1) * PART * PACK)
-            nc.vector.tensor_copy(
-                y_bf[:, wide].rearrange("p (c i t) -> p c t i", i=4, t=PACK),
-                src[:].rearrange("p t (c i) -> p c t i", i=4),
-            )
-            nc.vector.quantize_mx(y_codes[:, cols].bitcast(FP8X4), y_scales[:, cols], y_bf[:, wide])
+            quantise(y_codes[:, cols], y_scales[:, cols], y_bf[q][:])
 
-        last = PACK - 1
-        invert(slice(0, 3, 2))
+        def combine(rows):
+            nc.vector.tensor_tensor(share[:, rows], inverse[:, rows], fac4[:, rows], MULT)
+
+        def weigh_high(r):
+            nc.scalar.activation(w_rows[:, r, HALF:], expd[r][:, HALF:], COPY, scale=share[:, r : r + 1])
+
+        low = slice(0, HALF)
+        invert(1, 2)
         weigh(w_rows[:, 0, :], 0, slice(0, M))
-        invert(slice(1, 2))
-        weigh(w_rows[:, 2, :], 2, slice(0, M))
-        weigh(w_rows[:, 1, :], 1, slice(0, M))
-        turn_keys(3, ks_last, "bank1", 1)
-        warm = psum.tile([P, M], F32, name="warm", tag="bank3")
-        for r in range(2):
-            nc.tensor.matmul_mx(
-                warm[:],
-                lhsT=key_codes[r].bitcast(FP8X4),
-                lhsT_scale=key_scales[r],
-                rhs=cent_codes[:, :M].bitcast(FP8X4),
-                rhs_scale=cent_scales[:, :M],
-                start=True,
-                stop=True,
-            )
-        invert(slice(3, 4))
-        weave(0, last, nc.vector.tensor_copy)
-        weigh(w_bf[0][:, :, last], last, slice(0, PART))
+        invert(2, last)
+        weigh(w_rows[:, 1, low], 1, low)
+        combine(slice(1, last))
+        invert(last, PACK)
+        for r in range(1, last):
+            weigh_high(r)
+        weigh(w_rows[:, 2, low], 2, low)
+        weigh(w_bf[0].rearrange("s (m r) -> s m r", r=PACK)[:, :, last], last, slice(0, PART))
         weigh(w_rows[:, last, PART:], last, slice(PART, M))
+        nc.vector.tensor_copy(
+            w_bf[0].rearrange("s (c i r) -> s c r i", i=4, r=PACK)[:, :, :last, :],
+            w_rows[:, :last, :PART].rearrange("s r (c i) -> s c r i", i=4),
+        )
+        weave_w(nc.scalar.copy, 2)
+        weave_w(nc.scalar.copy, 3)
+        quantise_ks(last, PACK)
         quantise_w(0)
-        quantise_ks(1)
-        weave(2, PACK, nc.scalar.copy)
-        weave(1, PACK, nc.vector.tensor_copy)
-        weave(3, PACK, nc.scalar.copy)
-        banks = [product(0, range(PACK), "bank0", 1)]
-        for q, tag in ((1, "ksc_rows"), (2, "bank2")):
+        weave_w(nc.vector.tensor_copy, 1)
+        firsts = [product(0, range(2), "spare", 1), product(0, range(2, PACK), "ksc_rows", 1)]
+        order = (0, 2, 1, 3)
+        banks = {}
+        for q in order[1:-1]:
             quantise_w(q)
-            banks.append(product(q, range(PACK), tag, 1))
-        quantise_w(3)
-        halves = [product(3, range(2), "bank3", 1), product(3, range(2, PACK), "turned", 2)]
+            banks[q] = product(q, range(PACK), "bank%d" % (q - 1), 1)
+        quantise_w(order[-1])
+        lasts = [product(order[-1], range(2), "bank2", 1), product(order[-1], range(2, PACK), "bank3", 1)]
 
-        for q in range(parts):
-            if q < parts - 1:
-                nc.scalar.copy(y_rows[q][:], banks[q][:])
+        for q in order:
+            if q == order[0]:
+                for h in range(2):
+                    nc.scalar.copy(y_rows[q][:, 2 * h : 2 * h + 2, :], firsts[h][:])
+            elif q == order[-1]:
+                nc.scalar.copy(y_rows[q][:, :2, :], lasts[0][:])
+                nc.vector.tensor_copy(y_rows[q][:, 2:, :], lasts[1][:])
             else:
-                nc.scalar.copy(y_rows[q][:, :2, :], halves[0][:])
-                nc.vector.tensor_copy(y_rows[q][:, 2:, :], halves[1][:])
+                nc.scalar.copy(y_rows[q][:], banks[q][:])
             nc.sync.dma_start(out_rows[:, :, q * PART : (q + 1) * PART], y_rows[q][:])
-        for q in range(parts):
-            hand_on(q, y_rows[q])
+        for k in range(parts + 1):
+            if k < parts:
+                weave_y(order[k])
+            if k > 0:
+                quantise_y(order[k - 1])
         out_words = out_1.rearrange("z p m t -> p (z m t)").bitcast(I32)
-        for cols in (slice(0, early), slice(early, M)):
-            nc.sync.dma_start(out_words[:, cols], y_codes[:, cols].bitcast(I32))
+        nc.sync.dma_start(out_words, y_codes[:].bitcast(I32))
         for quad in range(4):
-            queue = nc.scalar if quad % 2 else nc.sync
+            queue = nc.sync if quad % 2 else nc.scalar
             queue.dma_start(
                 out_2[0, 4 * quad : 4 * quad + 4, :].bitcast(I32), y_scales[32 * quad : 32 * quad + 4, :].bitcast(I32)
             )

@@ -23,8 +23,8 @@ P = 128
 PACK = 4
 PART = 128
 HALF = 256
-SHARES = (192, 128)
-LAST_SHARE = 48
+SHARES = (224, 112)
+LAST_SHARE = 64
 
 
 def tile_attend_softcluster_pl_kernel(tc, keys, cent, fac, ksc, dsc, offs, out_0, out_1, out_2):
@@ -66,7 +66,6 @@ def tile_attend_softcluster_pl_kernel(tc, keys, cent, fac, ksc, dsc, offs, out_0
         fac4 = sb("fac4", [P, PACK], F32)
         nc.scalar.dma_start(ksc4[:], ksc.rearrange("(s r) o -> s (r o)", r=PACK))
         nc.scalar.dma_start(dsc4[:], dsc.rearrange("o (p t) -> p (o t)", t=PACK))
-        nc.scalar.dma_start(fac4[:], fac.rearrange("(s r) o -> s (r o)", r=PACK))
 
         identity = sb("identity", [P, P], F32)
         make_identity(nc, identity[:])
@@ -77,7 +76,7 @@ def tile_attend_softcluster_pl_kernel(tc, keys, cent, fac, ksc, dsc, offs, out_0
         picked = [sb("picked%d" % h, [P, 2, I], F32) for h in range(2)]
         key_bf = sb("key_bf", [P, PACK * P * PACK], BF16)
         ks_bf = sb("ks_bf", [P, PACK * 2 * P], F32)
-        ks_cols = [sb("ks_cols%d" % t, [P, I], BF16) for t in range(PACK - 1)]
+        ks_cols = [sb("ks_cols%d" % t, [P, I], BF16) for t in range(PACK)]
         nc.scalar.activation(picked[0][:, 1, ::HALF], dsc4[:, 0:1].to_broadcast([P, 2]), COPY)
         nc.scalar.activation(picked[1][:, :, ::HALF], dsc4[:, 1:3].unsqueeze(2).to_broadcast([P, 2, 2]), COPY)
 
@@ -115,18 +114,22 @@ def tile_attend_softcluster_pl_kernel(tc, keys, cent, fac, ksc, dsc, offs, out_0
                 picked[h][:, :, lo:hi].rearrange("p e (s r) -> p s r e", r=PACK),
             )
 
-        ks_codes = sb("ks_codes", [P, D], U32)
+        ks_codes = []
         ks_scales = sb("ks_scales", [P, D], U8)
 
-        def quantise_ks(lo, hi):
-            cols = slice(lo * P, hi * P)
-            quantise(ks_codes[:, cols], ks_scales[:, cols], ks_bf[:, lo * 2 * P : hi * 2 * P].bitcast(BF16))
+        def quantise_ks(h, tag):
+            ks_codes.append(sb("ks_codes%d" % h, [P, 2 * P], U32, tag))
+            quantise(
+                ks_codes[h][:],
+                ks_scales[:, h * 2 * P : (h + 1) * 2 * P],
+                ks_bf[:, h * PACK * P : (h + 1) * PACK * P].bitcast(BF16),
+            )
 
         for t in range(PACK - 1):
             for lo in (0, HALF):
                 gather(t, lo, lo + HALF)
             if t == 2:
-                quantise_ks(0, 2)
+                quantise_ks(0, "ks_codes0")
             for lo in (0, HALF):
                 scale_keys(t, lo, lo + HALF)
             turn_keys(t)
@@ -136,6 +139,7 @@ def tile_attend_softcluster_pl_kernel(tc, keys, cent, fac, ksc, dsc, offs, out_0
         for h in range(2):
             cent_raw.append(sb("cent_raw%d" % h, [P, PACK, HALF], F32))
             nc.sync.dma_start(cent_raw[h][:], cent_rows[:, :, h * HALF : (h + 1) * HALF])
+        nc.sync.dma_start(fac4[:], fac.rearrange("(s r) o -> s (r o)", r=PACK))
 
         key_codes = sb("key_codes", [P, PACK * P], U32)
         key_scales = sb("key_scales", [P, PACK * P], U8)
@@ -146,13 +150,15 @@ def tile_attend_softcluster_pl_kernel(tc, keys, cent, fac, ksc, dsc, offs, out_0
         gather(last, 0, HALF)
         gather(last, HALF, I)
         deal(nc.scalar.copy, 1, 0, HALF)
-        quantise_ks(2, 3)
+        scale_keys(last, 0, HALF)
         deal(nc.vector.tensor_copy, 1, HALF, I)
+        scale_keys(last, HALF, I)
 
         def weave_cent(h, tag):
             cut = SHARES[h]
             cent_bf.append(sb("cent_bf%d" % h, [P, HALF * PACK], BF16, tag))
-            weave(nc.vector.tensor_copy, cent_bf[h][:, cut * PACK :], cent_raw[h][:, :, cut:])
+            if cut < HALF:
+                weave(nc.vector.tensor_copy, cent_bf[h][:, cut * PACK :], cent_raw[h][:, :, cut:])
             weave(nc.scalar.copy, cent_bf[h][:, : cut * PACK], cent_raw[h][:, :, :cut])
 
         weave_cent(0, "pool3")
@@ -161,8 +167,8 @@ def tile_attend_softcluster_pl_kernel(tc, keys, cent, fac, ksc, dsc, offs, out_0
         for h in range(2):
             cols = slice(h * HALF, (h + 1) * HALF)
             quantise(cent_codes[:, cols], cent_scales[:, cols], cent_bf[h][:])
-        ks_cols.append(sb("ks_cols3", [P, I], BF16, "cent_raw0"))
-        scale_keys(last, 0, I)
+        turn_keys(last)
+        quantise_ks(1, "cent_raw0")
 
         scores = [psum.tile([P, M], F32, name="bank%d" % r) for r in range(PACK)]
         neg_max = [sb("neg_max%d" % r, [P, 1], F32) for r in range(PACK)]
@@ -170,7 +176,7 @@ def tile_attend_softcluster_pl_kernel(tc, keys, cent, fac, ksc, dsc, offs, out_0
         inverse = sb("inverse", [P, PACK], F32)
         expd = [sb("expd%d" % r, [P, M], F32) for r in range(PACK)]
         share = sb("share", [P, PACK], F32)
-        w_rows = sb("w_rows", [P, PACK, M], BF16)
+        w_rows = [sb("w_rows%d" % h, [P, PACK, HALF], BF16) for h in range(2)]
 
         def score(r, cols):
             slots = slice(r * P, (r + 1) * P)
@@ -189,7 +195,6 @@ def tile_attend_softcluster_pl_kernel(tc, keys, cent, fac, ksc, dsc, offs, out_0
                 invert(0, 1)
             nc.vector.tensor_reduce(neg_max[r][:], scores[r][:], AXIS_X, MAX, negate=True)
             nc.scalar.activation(expd[r][:], scores[r][:], EXP, bias=neg_max[r][:], accum_out=total[:, r : r + 1])
-        turn_keys(last)
         warm = psum.tile([P, M], F32, name="warm", tag="bank3")
         for r in range(2):
             slots = slice(r * P, (r + 1) * P)
@@ -208,7 +213,7 @@ def tile_attend_softcluster_pl_kernel(tc, keys, cent, fac, ksc, dsc, offs, out_0
             nc.vector.tensor_scalar(dst, expd[r][:, cols], inverse[:, r : r + 1], fac4[:, r : r + 1], MULT, MULT)
 
         def weave_w(move, q):
-            weave(move, w_bf[q], w_rows[:, :, q * PART : (q + 1) * PART])
+            weave(move, w_bf[q], w_rows[q // 2][:, :, q % 2 * PART : (q % 2 + 1) * PART])
 
         def quantise_w(q):
             quantise(w_codes[q][:], w_scales[q][:], w_bf[q])
@@ -217,7 +222,8 @@ def tile_attend_softcluster_pl_kernel(tc, keys, cent, fac, ksc, dsc, offs, out_0
             sums = psum.tile([P, len(planes), PART], F32, name="sums", tag=tag, bufs=bufs)
             for t in planes:
                 rows = slice(t * P, (t + 1) * P)
-                multiply(sums[:, t - planes[0], :], ks_codes[:, rows], ks_scales[:, rows], w_codes[q][:], w_scales[q][:])
+                codes = ks_codes[t // 2][:, t % 2 * P : (t % 2 + 1) * P]
+                multiply(sums[:, t - planes[0], :], codes, ks_scales[:, rows], w_codes[q][:], w_scales[q][:])
             return sums
 
         def weave_y(q):
@@ -234,47 +240,45 @@ def tile_attend_softcluster_pl_kernel(tc, keys, cent, fac, ksc, dsc, offs, out_0
             nc.vector.tensor_tensor(share[:, rows], inverse[:, rows], fac4[:, rows], MULT)
 
         def weigh_high(r):
-            nc.scalar.activation(w_rows[:, r, HALF:], expd[r][:, HALF:], COPY, scale=share[:, r : r + 1])
+            nc.scalar.activation(w_rows[1][:, r, :], expd[r][:, HALF:], COPY, scale=share[:, r : r + 1])
 
         low = slice(0, HALF)
+        high = slice(HALF, M)
         invert(1, 2)
-        weigh(w_rows[:, 0, :], 0, slice(0, M))
+        weigh(w_rows[0][:, 0, :], 0, low)
         invert(2, last)
-        weigh(w_rows[:, 1, low], 1, low)
-        combine(slice(1, last))
-        invert(last, PACK)
-        for r in range(1, last):
+        combine(slice(0, 2))
+        for r in range(2):
             weigh_high(r)
-        weigh(w_rows[:, 2, low], 2, low)
-        weigh(w_bf[0].rearrange("s (m r) -> s m r", r=PACK)[:, :, last], last, slice(0, PART))
-        weigh(w_rows[:, last, PART:], last, slice(PART, M))
+        weigh(w_rows[0][:, 1, :], 1, low)
+        weigh(w_rows[0][:, 2, :], 2, low)
+        invert(last, PACK)
+        for r in range(2, PACK):
+            weigh(w_rows[1][:, r, :], r, high)
         nc.vector.tensor_copy(
             w_bf[0].rearrange("s (c i r) -> s c r i", i=4, r=PACK)[:, :, :last, :],
-            w_rows[:, :last, :PART].rearrange("s r (c i) -> s c r i", i=4),
+            w_rows[0][:, :last, :PART].rearrange("s r (c i) -> s c r i", i=4),
         )
+        weigh(w_bf[0].rearrange("s (m r) -> s m r", r=PACK)[:, :, last], last, slice(0, PART))
+        weigh(w_rows[0][:, last, PART:], last, slice(PART, HALF))
         weave_w(nc.scalar.copy, 2)
         weave_w(nc.scalar.copy, 3)
-        quantise_ks(last, PACK)
         quantise_w(0)
         weave_w(nc.vector.tensor_copy, 1)
-        firsts = [product(0, range(2), "spare", 1), product(0, range(2, PACK), "ksc_rows", 1)]
         order = (0, 2, 1, 3)
-        banks = {}
-        for q in order[1:-1]:
+        banks = {0: [product(0, range(2), "spare", 1), product(0, range(2, PACK), "ksc_rows", 1)]}
+        quantise_w(2)
+        banks[2] = [product(2, range(2), "bank0", 1), product(2, range(2, PACK), "bank1", 1)]
+        for q, tag in ((1, "bank2"), (3, "bank3")):
             quantise_w(q)
-            banks[q] = product(q, range(PACK), "bank%d" % (q - 1), 1)
-        quantise_w(order[-1])
-        lasts = [product(order[-1], range(2), "bank2", 1), product(order[-1], range(2, PACK), "bank3", 1)]
+            banks[q] = [product(q, range(PACK), tag, 1)]
 
         for q in order:
-            if q == order[0]:
-                for h in range(2):
-                    nc.scalar.copy(y_rows[q][:, 2 * h : 2 * h + 2, :], firsts[h][:])
-            elif q == order[-1]:
-                nc.scalar.copy(y_rows[q][:, :2, :], lasts[0][:])
-                nc.vector.tensor_copy(y_rows[q][:, 2:, :], lasts[1][:])
+            if len(banks[q]) == 2:
+                nc.scalar.copy(y_rows[q][:, :2, :], banks[q][0][:])
+                nc.vector.tensor_copy(y_rows[q][:, 2:, :], banks[q][1][:])
             else:
-                nc.scalar.copy(y_rows[q][:], banks[q][:])
+                nc.scalar.copy(y_rows[q][:], banks[q][0][:])
             nc.sync.dma_start(out_rows[:, :, q * PART : (q + 1) * PART], y_rows[q][:])
         for k in range(parts + 1):
             if k < parts:

@@ -23,7 +23,7 @@ P = 128
 PACK = 4
 PART = 128
 HALF = 256
-SHARES = (224, 112)
+SHARES = (192, 160)
 LAST_SHARE = 64
 
 
@@ -75,7 +75,8 @@ def tile_attend_softcluster_pl_kernel(tc, keys, cent, fac, ksc, dsc, offs, out_0
 
         picked = [sb("picked%d" % h, [P, 2, I], F32) for h in range(2)]
         key_bf = sb("key_bf", [P, PACK * P * PACK], BF16)
-        ks_bf = sb("ks_bf", [P, PACK * 2 * P], F32)
+        ks_bf = sb("ks_bf", [P, (PACK - 1) * 2 * P], F32)
+        ks_planes = [ks_bf[:, t * 2 * P : (t + 1) * 2 * P] for t in range(PACK - 1)]
         ks_cols = [sb("ks_cols%d" % t, [P, I], BF16) for t in range(PACK)]
         nc.scalar.activation(picked[0][:, 1, ::HALF], dsc4[:, 0:1].to_broadcast([P, 2]), COPY)
         nc.scalar.activation(picked[1][:, :, ::HALF], dsc4[:, 1:3].unsqueeze(2).to_broadcast([P, 2, 2]), COPY)
@@ -103,8 +104,7 @@ def tile_attend_softcluster_pl_kernel(tc, keys, cent, fac, ksc, dsc, offs, out_0
             words = ks_cols[t][:].bitcast(F32)
             for u in range(2):
                 nc.tensor.transpose(turned[:, u, :], words[:, u::2], identity[:])
-            plane = ks_bf[:, t * 2 * P : (t + 1) * 2 * P]
-            nc.scalar.copy(plane.rearrange("s (p u) -> s p u", u=2), turned[:].rearrange("s u p -> s p u"))
+            nc.scalar.copy(ks_planes[t].rearrange("s (p u) -> s p u", u=2), turned[:].rearrange("s u p -> s p u"))
 
         def deal(move, h, lo, hi):
             move(
@@ -114,22 +114,17 @@ def tile_attend_softcluster_pl_kernel(tc, keys, cent, fac, ksc, dsc, offs, out_0
                 picked[h][:, :, lo:hi].rearrange("p e (s r) -> p s r e", r=PACK),
             )
 
-        ks_codes = []
+        ks_codes = sb("ks_codes", [P, D], U32)
         ks_scales = sb("ks_scales", [P, D], U8)
 
-        def quantise_ks(h, tag):
-            ks_codes.append(sb("ks_codes%d" % h, [P, 2 * P], U32, tag))
-            quantise(
-                ks_codes[h][:],
-                ks_scales[:, h * 2 * P : (h + 1) * 2 * P],
-                ks_bf[:, h * PACK * P : (h + 1) * PACK * P].bitcast(BF16),
-            )
+        def quantise_ks(lo, hi, values):
+            quantise(ks_codes[:, lo * P : hi * P], ks_scales[:, lo * P : hi * P], values.bitcast(BF16))
 
         for t in range(PACK - 1):
             for lo in (0, HALF):
                 gather(t, lo, lo + HALF)
             if t == 2:
-                quantise_ks(0, "ks_codes0")
+                quantise_ks(0, 2, ks_bf[:, : PACK * P])
             for lo in (0, HALF):
                 scale_keys(t, lo, lo + HALF)
             turn_keys(t)
@@ -141,7 +136,7 @@ def tile_attend_softcluster_pl_kernel(tc, keys, cent, fac, ksc, dsc, offs, out_0
             nc.sync.dma_start(cent_raw[h][:], cent_rows[:, :, h * HALF : (h + 1) * HALF])
         nc.sync.dma_start(fac4[:], fac.rearrange("(s r) o -> s (r o)", r=PACK))
 
-        key_codes = sb("key_codes", [P, PACK * P], U32)
+        first_codes = sb("first_codes", [P, P], U32)
         key_scales = sb("key_scales", [P, PACK * P], U8)
         cent_bf = []
         cent_codes = sb("cent_codes", [P, M], U32)
@@ -162,13 +157,23 @@ def tile_attend_softcluster_pl_kernel(tc, keys, cent, fac, ksc, dsc, offs, out_0
             weave(nc.scalar.copy, cent_bf[h][:, : cut * PACK], cent_raw[h][:, :, :cut])
 
         weave_cent(0, "pool3")
-        quantise(key_codes[:], key_scales[:], key_bf[:])
-        weave_cent(1, "cent_raw0")
+        quantise(first_codes[:], key_scales[:, :P], key_bf[:, : P * PACK])
+        weave_cent(1, "picked1")
         for h in range(2):
             cols = slice(h * HALF, (h + 1) * HALF)
             quantise(cent_codes[:, cols], cent_scales[:, cols], cent_bf[h][:])
+        ks_planes.append(sb("ks_last", [P, 2 * P], F32, "cent_raw1")[:])
         turn_keys(last)
-        quantise_ks(1, "cent_raw0")
+        later_codes = sb("later_codes", [P, last * P], U32, "picked1")
+        for lo, hi in ((1, 2), (2, PACK)):
+            quantise(
+                later_codes[:, (lo - 1) * P : (hi - 1) * P],
+                key_scales[:, lo * P : hi * P],
+                key_bf[:, lo * P * PACK : hi * P * PACK],
+            )
+        key_codes = [first_codes[:]] + [later_codes[:, r * P : (r + 1) * P] for r in range(last)]
+        for t in range(2, PACK):
+            quantise_ks(t, t + 1, ks_planes[t])
 
         scores = [psum.tile([P, M], F32, name="bank%d" % r) for r in range(PACK)]
         neg_max = [sb("neg_max%d" % r, [P, 1], F32) for r in range(PACK)]
@@ -180,7 +185,7 @@ def tile_attend_softcluster_pl_kernel(tc, keys, cent, fac, ksc, dsc, offs, out_0
 
         def score(r, cols):
             slots = slice(r * P, (r + 1) * P)
-            multiply(scores[r][:, cols], key_codes[:, slots], key_scales[:, slots], cent_codes[:, cols], cent_scales[:, cols])
+            multiply(scores[r][:, cols], key_codes[r], key_scales[:, slots], cent_codes[:, cols], cent_scales[:, cols])
 
         score(0, slice(0, HALF))
         score(0, slice(HALF, M))
@@ -198,7 +203,7 @@ def tile_attend_softcluster_pl_kernel(tc, keys, cent, fac, ksc, dsc, offs, out_0
         warm = psum.tile([P, M], F32, name="warm", tag="bank3")
         for r in range(2):
             slots = slice(r * P, (r + 1) * P)
-            multiply(warm[:], key_codes[:, slots], key_scales[:, slots], cent_codes[:], cent_scales[:])
+            multiply(warm[:], key_codes[r], key_scales[:, slots], cent_codes[:], cent_scales[:])
         parts = M // PART
         w_bf = [sb("w_bf%d" % q, [P, PART * PACK], BF16)[:] for q in range(parts)]
         w_codes = [sb("w_codes%d" % q, [P, PART], U32) for q in range(parts)]
@@ -222,8 +227,7 @@ def tile_attend_softcluster_pl_kernel(tc, keys, cent, fac, ksc, dsc, offs, out_0
             sums = psum.tile([P, len(planes), PART], F32, name="sums", tag=tag, bufs=bufs)
             for t in planes:
                 rows = slice(t * P, (t + 1) * P)
-                codes = ks_codes[t // 2][:, t % 2 * P : (t % 2 + 1) * P]
-                multiply(sums[:, t - planes[0], :], codes, ks_scales[:, rows], w_codes[q][:], w_scales[q][:])
+                multiply(sums[:, t - planes[0], :], ks_codes[:, rows], ks_scales[:, rows], w_codes[q][:], w_scales[q][:])
             return sums
 
         def weave_y(q):

@@ -23,7 +23,7 @@ P = 128
 PACK = 4
 PART = 128
 HALF = 256
-SHARES = (192, 160)
+SHARES = (128, 176)
 LAST_SHARE = 64
 
 
@@ -180,7 +180,7 @@ def tile_attend_softcluster_pl_kernel(tc, keys, cent, fac, ksc, dsc, offs, out_0
         total = sb("total", [P, PACK], F32)
         inverse = sb("inverse", [P, PACK], F32)
         expd = [sb("expd%d" % r, [P, M], F32) for r in range(PACK)]
-        share = sb("share", [P, PACK], F32)
+        share = sb("share", [P, 2], F32)
         w_rows = [sb("w_rows%d" % h, [P, PACK, HALF], BF16) for h in range(2)]
 
         def score(r, cols):
@@ -208,89 +208,96 @@ def tile_attend_softcluster_pl_kernel(tc, keys, cent, fac, ksc, dsc, offs, out_0
         w_bf = [sb("w_bf%d" % q, [P, PART * PACK], BF16)[:] for q in range(parts)]
         w_codes = [sb("w_codes%d" % q, [P, PART], U32) for q in range(parts)]
         w_scales = [sb("w_scales%d" % q, [P, PART], U8) for q in range(parts)]
-        y_rows = [sb("y_rows%d" % q, [P, PACK, PART], F32) for q in range(parts)]
+        y_rows = [sb("y_rows%d" % h, [P, PACK, HALF], F32) for h in range(2)]
         y_bf = [sb("y_bf%d" % q, [P, PART * PACK], BF16) for q in range(parts)]
         y_codes = sb("y_codes", [P, M], U32)
         y_scales = sb("y_scales", [P, M], U8)
         out_rows = out_0.rearrange("(p t) m -> p t m", t=PACK)
+        out_words = out_1.rearrange("z p m t -> p (z m t)").bitcast(I32)
 
-        def weigh(dst, r, cols):
-            nc.vector.tensor_scalar(dst, expd[r][:, cols], inverse[:, r : r + 1], fac4[:, r : r + 1], MULT, MULT)
+        def weigh(dst, r, src):
+            nc.vector.tensor_scalar(dst, src, inverse[:, r : r + 1], fac4[:, r : r + 1], MULT, MULT)
+
+        def every_other(r, odd):
+            return expd[r][:].rearrange("s (h e m) -> s h e m", h=2, e=2)[:, :, odd, :]
+
+        def weigh_rows(r, odd):
+            weigh(w_rows[odd][:, r, :].rearrange("s (h m) -> s h m", h=2), r, every_other(r, odd))
+
+        def weigh_odd(r):
+            dst = w_rows[1][:, r, :].rearrange("s (h m) -> s h m", h=2)
+            nc.scalar.activation(dst, every_other(r, 1), COPY, scale=share[:, r : r + 1])
 
         def weave_w(move, q):
-            weave(move, w_bf[q], w_rows[q // 2][:, :, q % 2 * PART : (q % 2 + 1) * PART])
+            weave(move, w_bf[q], w_rows[q % 2][:, :, q // 2 * PART : (q // 2 + 1) * PART])
 
         def quantise_w(q):
             quantise(w_codes[q][:], w_scales[q][:], w_bf[q])
 
-        def product(q, planes, tag, bufs):
-            sums = psum.tile([P, len(planes), PART], F32, name="sums", tag=tag, bufs=bufs)
+        def product(q, planes, tag):
+            sums = psum.tile([P, len(planes), PART], F32, name="sums", tag=tag, bufs=1)
             for t in planes:
                 rows = slice(t * P, (t + 1) * P)
                 multiply(sums[:, t - planes[0], :], ks_codes[:, rows], ks_scales[:, rows], w_codes[q][:], w_scales[q][:])
             return sums
 
+        def y_part(q):
+            return y_rows[q // 2][:, :, q % 2 * PART : (q % 2 + 1) * PART]
+
         def weave_y(q):
             cut = LAST_SHARE if q == parts - 1 else 0
-            weave(nc.vector.tensor_copy, y_bf[q][:, cut * PACK :], y_rows[q][:, :, cut:])
+            weave(nc.vector.tensor_copy, y_bf[q][:, cut * PACK :], y_part(q)[:, :, cut:])
             if cut:
-                weave(nc.scalar.copy, y_bf[q][:, : cut * PACK], y_rows[q][:, :, :cut])
+                weave(nc.scalar.copy, y_bf[q][:, : cut * PACK], y_part(q)[:, :, :cut])
 
         def quantise_y(q):
             cols = slice(q * PART, (q + 1) * PART)
             quantise(y_codes[:, cols], y_scales[:, cols], y_bf[q][:])
 
-        def combine(rows):
-            nc.vector.tensor_tensor(share[:, rows], inverse[:, rows], fac4[:, rows], MULT)
-
-        def weigh_high(r):
-            nc.scalar.activation(w_rows[1][:, r, :], expd[r][:, HALF:], COPY, scale=share[:, r : r + 1])
-
-        low = slice(0, HALF)
-        high = slice(HALF, M)
         invert(1, 2)
-        weigh(w_rows[0][:, 0, :], 0, low)
+        weigh_rows(0, 0)
         invert(2, last)
-        combine(slice(0, 2))
+        nc.vector.tensor_tensor(share[:], inverse[:, :2], fac4[:, :2], MULT)
         for r in range(2):
-            weigh_high(r)
-        weigh(w_rows[0][:, 1, :], 1, low)
-        weigh(w_rows[0][:, 2, :], 2, low)
+            weigh_odd(r)
+        weigh_rows(1, 0)
+        weigh_rows(2, 0)
         invert(last, PACK)
         for r in range(2, PACK):
-            weigh(w_rows[1][:, r, :], r, high)
+            weigh_rows(r, 1)
         nc.vector.tensor_copy(
             w_bf[0].rearrange("s (c i r) -> s c r i", i=4, r=PACK)[:, :, :last, :],
             w_rows[0][:, :last, :PART].rearrange("s r (c i) -> s c r i", i=4),
         )
-        weigh(w_bf[0].rearrange("s (m r) -> s m r", r=PACK)[:, :, last], last, slice(0, PART))
-        weigh(w_rows[0][:, last, PART:], last, slice(PART, HALF))
-        weave_w(nc.scalar.copy, 2)
+        weigh(w_bf[0].rearrange("s (m r) -> s m r", r=PACK)[:, :, last], last, expd[last][:, :PART])
+        weigh(w_rows[0][:, last, PART:], last, expd[last][:, HALF : HALF + PART])
+        weave_w(nc.scalar.copy, 1)
         weave_w(nc.scalar.copy, 3)
         quantise_w(0)
-        weave_w(nc.vector.tensor_copy, 1)
-        order = (0, 2, 1, 3)
-        banks = {0: [product(0, range(2), "spare", 1), product(0, range(2, PACK), "ksc_rows", 1)]}
-        quantise_w(2)
-        banks[2] = [product(2, range(2), "bank0", 1), product(2, range(2, PACK), "bank1", 1)]
-        for q, tag in ((1, "bank2"), (3, "bank3")):
+        weave_w(nc.vector.tensor_copy, 2)
+        banks = [[product(0, range(2), "spare"), product(0, range(2, PACK), "ksc_rows")]]
+        quantise_w(1)
+        banks.append([product(1, range(2), "bank0"), product(1, range(2, PACK), "bank1")])
+        for q in range(2, parts):
             quantise_w(q)
-            banks[q] = [product(q, range(PACK), tag, 1)]
+            banks.append([product(q, range(PACK), "bank%d" % q)])
 
-        for q in order:
+        for q in range(parts):
             if len(banks[q]) == 2:
-                nc.scalar.copy(y_rows[q][:, :2, :], banks[q][0][:])
-                nc.vector.tensor_copy(y_rows[q][:, 2:, :], banks[q][1][:])
+                nc.scalar.copy(y_part(q)[:, :2, :], banks[q][0][:])
+                nc.vector.tensor_copy(y_part(q)[:, 2:, :], banks[q][1][:])
             else:
-                nc.scalar.copy(y_rows[q][:], banks[q][0][:])
-            nc.sync.dma_start(out_rows[:, :, q * PART : (q + 1) * PART], y_rows[q][:])
-        for k in range(parts + 1):
-            if k < parts:
-                weave_y(order[k])
-            if k > 0:
-                quantise_y(order[k - 1])
-        out_words = out_1.rearrange("z p m t -> p (z m t)").bitcast(I32)
-        nc.sync.dma_start(out_words, y_codes[:].bitcast(I32))
+                nc.scalar.copy(y_part(q), banks[q][0][:])
+            if q < 2:
+                nc.sync.dma_start(out_rows[:, :, q * PART : (q + 1) * PART], y_part(q))
+        for h in range(2):
+            for step in (weave_y, quantise_y):
+                step(2 * h)
+                step(2 * h + 1)
+            cols = slice(h * HALF, (h + 1) * HALF)
+            nc.sync.dma_start(out_words[:, cols], y_codes[:, cols].bitcast(I32))
+            if h == 0:
+                nc.sync.dma_start(out_rows[:, :, HALF:], y_rows[1][:])
         for quad in range(4):
             queue = nc.sync if quad % 2 else nc.scalar
             queue.dma_start(

@@ -24,7 +24,7 @@ PACK = 4
 PART = 128
 HALF = 256
 SHARES = (128, 176)
-LAST_SHARE = 64
+LAST_SHARE = 112
 
 
 def tile_attend_softcluster_pl_kernel(tc, keys, cent, fac, ksc, dsc, offs, out_0, out_1, out_2):
@@ -278,26 +278,32 @@ def tile_attend_softcluster_pl_kernel(tc, keys, cent, fac, ksc, dsc, offs, out_0
         banks = [[product(0, range(2), "spare"), product(0, range(2, PACK), "ksc_rows")]]
         quantise_w(1)
         banks.append([product(1, range(2), "bank0"), product(1, range(2, PACK), "bank1")])
-        for q in range(2, parts):
-            quantise_w(q)
-            banks.append([product(q, range(PACK), "bank%d" % q)])
 
-        for q in range(parts):
+        def fetch(q):
             if len(banks[q]) == 2:
-                nc.scalar.copy(y_part(q)[:, :2, :], banks[q][0][:])
-                nc.vector.tensor_copy(y_part(q)[:, 2:, :], banks[q][1][:])
+                nc.vector.tensor_copy(y_part(q)[:, :2, :], banks[q][0][:])
+                nc.scalar.copy(y_part(q)[:, 2:, :], banks[q][1][:])
             else:
                 nc.scalar.copy(y_part(q), banks[q][0][:])
             if q < 2:
                 nc.sync.dma_start(out_rows[:, :, q * PART : (q + 1) * PART], y_part(q))
+
+        for q in range(2, parts):
+            quantise_w(q)
+            if q == 2:
+                banks.append([product(q, range(PACK), "bank2")])
+                fetch(0)
+            else:
+                banks.append([product(q, range(2), "bank3"), product(q, range(2, PACK), "spare")])
+        for q in range(1, parts):
+            fetch(q)
         for h in range(2):
             for step in (weave_y, quantise_y):
                 step(2 * h)
                 step(2 * h + 1)
-            cols = slice(h * HALF, (h + 1) * HALF)
-            nc.sync.dma_start(out_words[:, cols], y_codes[:, cols].bitcast(I32))
             if h == 0:
                 nc.sync.dma_start(out_rows[:, :, HALF:], y_rows[1][:])
+        nc.sync.dma_start(out_words, y_codes[:].bitcast(I32))
         for quad in range(4):
             queue = nc.sync if quad % 2 else nc.scalar
             queue.dma_start(

@@ -200,8 +200,8 @@ def tile_attend_softcluster_pl_kernel(tc, keys, cent, fac, ksc, dsc, offs, out_0
                 invert(0, 1)
             nc.vector.tensor_reduce(neg_max[r][:], scores[r][:], AXIS_X, MAX, negate=True)
             nc.scalar.activation(expd[r][:], scores[r][:], EXP, bias=neg_max[r][:], accum_out=total[:, r : r + 1])
-        warm = psum.tile([P, M], F32, name="warm", tag="bank3")
         for r in range(2):
+            warm = psum.tile([P, M], F32, name="warm", tag="bank%d" % (r + 2))
             slots = slice(r * P, (r + 1) * P)
             multiply(warm[:], key_codes[r], key_scales[:, slots], cent_codes[:], cent_scales[:])
         parts = M // PART

@@ -200,10 +200,6 @@ def tile_attend_softcluster_pl_kernel(tc, keys, cent, fac, ksc, dsc, offs, out_0
                 invert(0, 1)
             nc.vector.tensor_reduce(neg_max[r][:], scores[r][:], AXIS_X, MAX, negate=True)
             nc.scalar.activation(expd[r][:], scores[r][:], EXP, bias=neg_max[r][:], accum_out=total[:, r : r + 1])
-        for r in range(2):
-            warm = psum.tile([P, M], F32, name="warm", tag="bank%d" % (r + 2))
-            slots = slice(r * P, (r + 1) * P)
-            multiply(warm[:], key_codes[r], key_scales[:, slots], cent_codes[:], cent_scales[:])
         parts = M // PART
         w_bf = [sb("w_bf%d" % q, [P, PART * PACK], BF16)[:] for q in range(parts)]
         w_codes = [sb("w_codes%d" % q, [P, PART], U32) for q in range(parts)]

@@ -23,7 +23,7 @@ P = 128
 PACK = 4
 PART = 128
 HALF = 256
-SHARES = (128, 176)
+SHARES = (160, 96)
 LAST_SHARE = 112
 
 
@@ -31,7 +31,11 @@ def tile_attend_softcluster_pl_kernel(tc, keys, cent, fac, ksc, dsc, offs, out_0
     nc = tc.nc
     with ExitStack() as ctx:
         keep = ctx.enter_context(tc.tile_pool(name="keep", bufs=1))
+        reuse = ctx.enter_context(tc.tile_pool(name="reuse", bufs=1))
         psum = ctx.enter_context(tc.psum_pool(name="psum", bufs=1))
+
+        def placed(name, shape, dtype, offset):
+            return reuse.tile(shape, dtype, name=name, align_bytes=64, offset=offset)
 
         def sb(name, shape, dtype, tag=None):
             return keep.tile(shape, dtype, name=name, tag=tag or name, align_bytes=64)
@@ -75,15 +79,13 @@ def tile_attend_softcluster_pl_kernel(tc, keys, cent, fac, ksc, dsc, offs, out_0
 
         picked = [sb("picked%d" % h, [P, 2, I], F32) for h in range(2)]
         key_bf = sb("key_bf", [P, PACK * P * PACK], BF16)
-        ks_bf = sb("ks_bf", [P, (PACK - 1) * 2 * P], F32)
-        ks_planes = [ks_bf[:, t * 2 * P : (t + 1) * 2 * P] for t in range(PACK - 1)]
-        ks_cols = [sb("ks_cols%d" % t, [P, I], BF16) for t in range(PACK)]
+        ks_bf = sb("ks_bf", [P, 2 * 2 * P], F32)
+        ks_planes = [ks_bf[:, t * 2 * P : (t + 1) * 2 * P] for t in range(2)]
+        ks_cols = [sb("ks_cols%d" % t, [P, I], BF16) for t in range(PACK - 1)]
         nc.scalar.activation(picked[0][:, 1, ::HALF], dsc4[:, 0:1].to_broadcast([P, 2]), COPY)
         nc.scalar.activation(picked[1][:, :, ::HALF], dsc4[:, 1:3].unsqueeze(2).to_broadcast([P, 2, 2]), COPY)
 
         def factor(t, lo):
-            if t == PACK - 1:
-                return dsc4[:, t : t + 1]
             return picked[(t + 1) // 2][:, (t + 1) % 2, lo : lo + 1]
 
         def gather(t, lo, hi):
@@ -104,7 +106,10 @@ def tile_attend_softcluster_pl_kernel(tc, keys, cent, fac, ksc, dsc, offs, out_0
             words = ks_cols[t][:].bitcast(F32)
             for u in range(2):
                 nc.tensor.transpose(turned[:, u, :], words[:, u::2], identity[:])
-            nc.scalar.copy(ks_planes[t].rearrange("s (p u) -> s p u", u=2), turned[:].rearrange("s u p -> s p u"))
+            return turned
+
+        def fetch_keys(dst, turned):
+            nc.scalar.copy(dst.rearrange("s (p u) -> s p u", u=2), turned[:].rearrange("s u p -> s p u"))
 
         def deal(move, h, lo, hi):
             move(
@@ -127,27 +132,33 @@ def tile_attend_softcluster_pl_kernel(tc, keys, cent, fac, ksc, dsc, offs, out_0
                 quantise_ks(0, 2, ks_bf[:, : PACK * P])
             for lo in (0, HALF):
                 scale_keys(t, lo, lo + HALF)
-            turn_keys(t)
+            turned = turn_keys(t)
+            if t < 2:
+                fetch_keys(ks_planes[t], turned)
             if t == 1:
                 deal(nc.scalar.copy, 0, 0, I)
         cent_raw = []
         for h in range(2):
-            cent_raw.append(sb("cent_raw%d" % h, [P, PACK, HALF], F32))
+            cent_raw.append(placed("cent_raw%d" % h, [P, PACK, HALF], F32, h * 4096))
             nc.sync.dma_start(cent_raw[h][:], cent_rows[:, :, h * HALF : (h + 1) * HALF])
         nc.sync.dma_start(fac4[:], fac.rearrange("(s r) o -> s (r o)", r=PACK))
 
         first_codes = sb("first_codes", [P, P], U32)
         key_scales = sb("key_scales", [P, PACK * P], U8)
         cent_bf = []
-        cent_codes = sb("cent_codes", [P, M], U32)
         cent_scales = sb("cent_scales", [P, M], U8)
         last = PACK - 1
-        gather(last, 0, HALF)
-        gather(last, HALF, I)
-        deal(nc.scalar.copy, 1, 0, HALF)
-        scale_keys(last, 0, HALF)
-        deal(nc.vector.tensor_copy, 1, HALF, I)
-        scale_keys(last, HALF, I)
+        nc.scalar.activation(picked[1][:, 1, :HALF], pool[last][:].indirect(offsets[:, : HALF // 16]), COPY)
+        gather(last, HALF, HALF + PART)
+        gather(last, HALF + PART, I)
+        deal(nc.vector.tensor_copy, 1, HALF, HALF + PART)
+        deal(nc.vector.tensor_copy, 1, HALF + PART, I)
+        deal(nc.vector.tensor_copy, 1, 0, HALF)
+        last_scaled = sb("last_scaled", [P, I], F32)
+        nc.scalar.activation(last_scaled[:], picked[1][:, 1, :], COPY, scale=dsc4[:, last:])
+        last_turned = psum.tile([P, PACK, P], F32, name="last_turned", tag="turned", bufs=2)
+        for r in range(PACK):
+            nc.tensor.transpose(last_turned[:, r, :], last_scaled[:, r::PACK], identity[:])
 
         def weave_cent(h, tag):
             cut = SHARES[h]
@@ -159,11 +170,17 @@ def tile_attend_softcluster_pl_kernel(tc, keys, cent, fac, ksc, dsc, offs, out_0
         weave_cent(0, "pool3")
         quantise(first_codes[:], key_scales[:, :P], key_bf[:, : P * PACK])
         weave_cent(1, "picked1")
+        cent_codes = placed("cent_codes", [P, M], U32, 4096 + 3072)
         for h in range(2):
             cols = slice(h * HALF, (h + 1) * HALF)
             quantise(cent_codes[:, cols], cent_scales[:, cols], cent_bf[h][:])
-        ks_planes.append(sb("ks_last", [P, 2 * P], F32, "cent_raw1")[:])
-        turn_keys(last)
+        ks_late = placed("ks_late", [P, 3 * 2 * P], F32, 4096)
+        fetch_keys(ks_late[:, : 2 * P], turned)
+        last_rows = ks_late[:, 2 * P : 4 * P].bitcast(BF16)
+        last_bf = ks_late[:, 4 * P :]
+        for r in range(PACK):
+            nc.scalar.activation(last_rows[:, r * P : (r + 1) * P], last_turned[:, r, :], COPY, scale=ksc4[:, r : r + 1])
+        weave(nc.scalar.copy, last_bf.bitcast(BF16), last_rows.rearrange("s (r p) -> s r p", r=PACK))
         later_codes = sb("later_codes", [P, last * P], U32, "picked1")
         for lo, hi in ((1, 2), (2, PACK)):
             quantise(
@@ -172,8 +189,7 @@ def tile_attend_softcluster_pl_kernel(tc, keys, cent, fac, ksc, dsc, offs, out_0
                 key_bf[:, lo * P * PACK : hi * P * PACK],
             )
         key_codes = [first_codes[:]] + [later_codes[:, r * P : (r + 1) * P] for r in range(last)]
-        for t in range(2, PACK):
-            quantise_ks(t, t + 1, ks_planes[t])
+        quantise_ks(2, 3, ks_late[:, : 2 * P])
 
         scores = [psum.tile([P, M], F32, name="bank%d" % r) for r in range(PACK)]
         neg_max = [sb("neg_max%d" % r, [P, 1], F32) for r in range(PACK)]
@@ -200,7 +216,9 @@ def tile_attend_softcluster_pl_kernel(tc, keys, cent, fac, ksc, dsc, offs, out_0
                 invert(0, 1)
             nc.vector.tensor_reduce(neg_max[r][:], scores[r][:], AXIS_X, MAX, negate=True)
             nc.scalar.activation(expd[r][:], scores[r][:], EXP, bias=neg_max[r][:], accum_out=total[:, r : r + 1])
+        quantise_ks(last, PACK, last_bf)
         parts = M // PART
+
         w_bf = [sb("w_bf%d" % q, [P, PART * PACK], BF16)[:] for q in range(parts)]
         w_codes = [sb("w_codes%d" % q, [P, PART], U32) for q in range(parts)]
         w_scales = [sb("w_scales%d" % q, [P, PART], U8) for q in range(parts)]

@@ -113,10 +113,10 @@ def tile_attend_softcluster_pl_kernel(tc, keys, cent, fac, ksc, dsc, offs, out_0
 
         def deal(move, h, lo, hi):
             move(
-                key_bf[:].rearrange("p (r s t) -> p s r t", r=PACK, t=PACK)[
-                    :, lo // PACK : hi // PACK, :, 2 * h : 2 * h + 2
+                key_bf[:].rearrange("p (r c i t) -> p c r i t", r=PACK, i=2, t=PACK)[
+                    :, lo // 8 : hi // 8, :, :, 2 * h : 2 * h + 2
                 ],
-                picked[h][:, :, lo:hi].rearrange("p e (s r) -> p s r e", r=PACK),
+                picked[h][:, :, lo:hi].rearrange("p e (c i r) -> p c r i e", i=2, r=PACK),
             )
 
         ks_codes = sb("ks_codes", [P, D], U32)
@@ -128,8 +128,8 @@ def tile_attend_softcluster_pl_kernel(tc, keys, cent, fac, ksc, dsc, offs, out_0
         for t in range(PACK - 1):
             for lo in (0, HALF):
                 gather(t, lo, lo + HALF)
-            if t == 2:
-                quantise_ks(0, 2, ks_bf[:, : PACK * P])
+            if t > 0:
+                quantise_ks(t - 1, t, ks_planes[t - 1])
             for lo in (0, HALF):
                 scale_keys(t, lo, lo + HALF)
             turned = turn_keys(t)

from contextlib import ExitStack

import concourse.mybir as mybir
from concourse.masks import make_identity

D, T, I, M = 512, 2048, 512, 512
FLOPS = 2 * 2 * D * I * M

F32 = mybir.dt.float32
BF16 = mybir.dt.bfloat16
I32 = mybir.dt.int32
U32 = mybir.dt.uint32
U16 = mybir.dt.uint16
U8 = mybir.dt.uint8
FP8X4 = mybir.dt.float8_e4m3fn_x4
MULT = mybir.AluOpType.mult
MAX = mybir.AluOpType.max
COPY = mybir.ActivationFunctionType.Copy
EXP = mybir.ActivationFunctionType.Exp
AXIS_X = mybir.AxisListType.X

P = 128
PACK = 4
PART = 128
HALF = 256
SHARES = (160, 96)
LAST_SHARE = 112


def tile_attend_softcluster_pl_kernel(tc, keys, cent, fac, ksc, dsc, offs, out_0, out_1, out_2):
    nc = tc.nc
    with ExitStack() as ctx:
        keep = ctx.enter_context(tc.tile_pool(name="keep", bufs=1))
        reuse = ctx.enter_context(tc.tile_pool(name="reuse", bufs=1))
        psum = ctx.enter_context(tc.psum_pool(name="psum", bufs=1))

        def placed(name, shape, dtype, offset):
            return reuse.tile(shape, dtype, name=name, align_bytes=64, offset=offset)

        def sb(name, shape, dtype, tag=None):
            return keep.tile(shape, dtype, name=name, tag=tag or name, align_bytes=64)

        def quantise(codes, scales, values):
            nc.vector.quantize_mx(codes.bitcast(FP8X4), scales, values)

        def multiply(out, lhs_codes, lhs_scales, rhs_codes, rhs_scales):
            nc.tensor.matmul_mx(
                out,
                lhsT=lhs_codes.bitcast(FP8X4),
                lhsT_scale=lhs_scales,
                rhs=rhs_codes.bitcast(FP8X4),
                rhs_scale=rhs_scales,
                start=True,
                stop=True,
            )

        def weave(move, dst, src):
            move(dst.rearrange("p (c i t) -> p c t i", i=4, t=PACK), src.rearrange("p t (c i) -> p c t i", i=4))

        offsets = keep.tile([P, I // 16], U16, name="offsets")
        cent_rows = cent.rearrange("(p t) m -> p t m", t=PACK)
        key_rows = keys.rearrange("(p t) n -> p t n", t=PACK)
        pool = [sb("pool%d" % t, [P, T], F32) for t in range(PACK)]
        nc.sync.dma_start(pool[0][:], key_rows[:, 0, :])
        nc.sync.dma_start(offsets[:], offs)
        for t in range(1, PACK):
            nc.sync.dma_start(pool[t][:], key_rows[:, t, :])
        ksc4 = sb("ksc4", [P, PACK], F32)
        dsc4 = sb("dsc4", [P, PACK], F32)
        fac4 = sb("fac4", [P, PACK], F32)
        nc.scalar.dma_start(ksc4[:], ksc.rearrange("(s r) o -> s (r o)", r=PACK))
        nc.scalar.dma_start(dsc4[:], dsc.rearrange("o (p t) -> p (o t)", t=PACK))

        identity = sb("identity", [P, P], F32)
        make_identity(nc, identity[:])
        ksc_rows = psum.tile([P, PACK, P], F32, name="ksc_rows")
        for r in range(PACK):
            nc.tensor.transpose(ksc_rows[:, r, :], ksc4[:, r : r + 1].to_broadcast([P, P]), identity[:])

        picked = [sb("picked%d" % h, [P, 2, I], F32) for h in range(2)]
        key_bf = sb("key_bf", [P, PACK * P * PACK], BF16)
        ks_bf = sb("ks_bf", [P, 2 * 2 * P], F32)
        ks_planes = [ks_bf[:, t * 2 * P : (t + 1) * 2 * P] for t in range(2)]
        ks_cols = [sb("ks_cols%d" % t, [P, I], BF16) for t in range(PACK - 1)]
        nc.scalar.activation(picked[0][:, 1, ::HALF], dsc4[:, 0:1].to_broadcast([P, 2]), COPY)
        nc.scalar.activation(picked[1][:, :, ::HALF], dsc4[:, 1:3].unsqueeze(2).to_broadcast([P, 2, 2]), COPY)

        def factor(t, lo):
            return picked[(t + 1) // 2][:, (t + 1) % 2, lo : lo + 1]

        def gather(t, lo, hi):
            nc.vector.tensor_copy(picked[t // 2][:, t % 2, lo:hi], pool[t][:].indirect(offsets[:, lo // 16 : hi // 16]))

        def scale_keys(t, lo, hi):
            nc.vector.scalar_tensor_tensor(
                ks_cols[t][:, lo:hi].rearrange("p (s r) -> p s r", r=PACK),
                picked[t // 2][:, t % 2, lo:hi].rearrange("p (s r) -> p s r", r=PACK),
                factor(t, lo),
                ksc_rows[:, :, lo // PACK : hi // PACK].rearrange("p r s -> p s r"),
                MULT,
                MULT,
            )

        def turn_keys(t):
            turned = psum.tile([P, 2, P], F32, name="turned", tag="turned", bufs=2)
            words = ks_cols[t][:].bitcast(F32)
            for u in range(2):
                nc.tensor.transpose(turned[:, u, :], words[:, u::2], identity[:])
            return turned

        def fetch_keys(dst, turned):
            nc.scalar.copy(dst.rearrange("s (p u) -> s p u", u=2), turned[:].rearrange("s u p -> s p u"))

        def deal(move, h, lo, hi):
            move(
                key_bf[:].rearrange("p (r c i t) -> p c r i t", r=PACK, i=2, t=PACK)[
                    :, lo // 8 : hi // 8, :, :, 2 * h : 2 * h + 2
                ],
                picked[h][:, :, lo:hi].rearrange("p e (c i r) -> p c r i e", i=2, r=PACK),
            )

        ks_codes = sb("ks_codes", [P, D], U32)
        ks_scales = sb("ks_scales", [P, D], U8)

        def quantise_ks(lo, hi, values):
            quantise(ks_codes[:, lo * P : hi * P], ks_scales[:, lo * P : hi * P], values.bitcast(BF16))

        for t in range(PACK - 1):
            for lo in (0, HALF):
                gather(t, lo, lo + HALF)
            if t > 0:
                quantise_ks(t - 1, t, ks_planes[t - 1])
            for lo in (0, HALF):
                scale_keys(t, lo, lo + HALF)
            turned = turn_keys(t)
            if t < 2:
                fetch_keys(ks_planes[t], turned)
            if t == 1:
                deal(nc.scalar.copy, 0, 0, I)
        cent_raw = []
        for h in range(2):
            cent_raw.append(placed("cent_raw%d" % h, [P, PACK, HALF], F32, h * 4096))
            nc.sync.dma_start(cent_raw[h][:], cent_rows[:, :, h * HALF : (h + 1) * HALF])
        nc.sync.dma_start(fac4[:], fac.rearrange("(s r) o -> s (r o)", r=PACK))

        first_codes = sb("first_codes", [P, P], U32)
        key_scales = sb("key_scales", [P, PACK * P], U8)
        cent_bf = []
        cent_scales = sb("cent_scales", [P, M], U8)
        last = PACK - 1
        nc.scalar.activation(picked[1][:, 1, :HALF], pool[last][:].indirect(offsets[:, : HALF // 16]), COPY)
        gather(last, HALF, HALF + PART)
        gather(last, HALF + PART, I)
        deal(nc.vector.tensor_copy, 1, HALF, HALF + PART)
        deal(nc.vector.tensor_copy, 1, HALF + PART, I)
        deal(nc.vector.tensor_copy, 1, 0, HALF)
        last_scaled = sb("last_scaled", [P, I], F32)
        nc.scalar.activation(last_scaled[:], picked[1][:, 1, :], COPY, scale=dsc4[:, last:])
        last_turned = psum.tile([P, PACK, P], F32, name="last_turned", tag="turned", bufs=2)
        for r in range(PACK):
            nc.tensor.transpose(last_turned[:, r, :], last_scaled[:, r::PACK], identity[:])

        def weave_cent(h, tag):
            cut = SHARES[h]
            cent_bf.append(sb("cent_bf%d" % h, [P, HALF * PACK], BF16, tag))
            if cut < HALF:
                weave(nc.vector.tensor_copy, cent_bf[h][:, cut * PACK :], cent_raw[h][:, :, cut:])
            weave(nc.scalar.copy, cent_bf[h][:, : cut * PACK], cent_raw[h][:, :, :cut])

        weave_cent(0, "pool3")
        quantise(first_codes[:], key_scales[:, :P], key_bf[:, : P * PACK])
        weave_cent(1, "picked1")
        cent_codes = placed("cent_codes", [P, M], U32, 4096 + 3072)
        for h in range(2):
            cols = slice(h * HALF, (h + 1) * HALF)
            quantise(cent_codes[:, cols], cent_scales[:, cols], cent_bf[h][:])
        ks_late = placed("ks_late", [P, 3 * 2 * P], F32, 4096)
        fetch_keys(ks_late[:, : 2 * P], turned)
        last_rows = ks_late[:, 2 * P : 4 * P].bitcast(BF16)
        last_bf = ks_late[:, 4 * P :]
        for r in range(PACK):
            nc.scalar.activation(last_rows[:, r * P : (r + 1) * P], last_turned[:, r, :], COPY, scale=ksc4[:, r : r + 1])
        weave(nc.scalar.copy, last_bf.bitcast(BF16), last_rows.rearrange("s (r p) -> s r p", r=PACK))
        later_codes = sb("later_codes", [P, last * P], U32, "picked1")
        for lo, hi in ((1, 2), (2, PACK)):
            quantise(
                later_codes[:, (lo - 1) * P : (hi - 1) * P],
                key_scales[:, lo * P : hi * P],
                key_bf[:, lo * P * PACK : hi * P * PACK],
            )
        key_codes = [first_codes[:]] + [later_codes[:, r * P : (r + 1) * P] for r in range(last)]
        quantise_ks(2, 3, ks_late[:, : 2 * P])

        scores = [psum.tile([P, M], F32, name="bank%d" % r) for r in range(PACK)]
        neg_max = [sb("neg_max%d" % r, [P, 1], F32) for r in range(PACK)]
        total = sb("total", [P, PACK], F32)
        inverse = sb("inverse", [P, PACK], F32)
        expd = [sb("expd%d" % r, [P, M], F32) for r in range(PACK)]
        share = sb("share", [P, 2], F32)
        w_rows = [sb("w_rows%d" % h, [P, PACK, HALF], BF16) for h in range(2)]

        def score(r, cols):
            slots = slice(r * P, (r + 1) * P)
            multiply(scores[r][:, cols], key_codes[r], key_scales[:, slots], cent_codes[:, cols], cent_scales[:, cols])

        score(0, slice(0, HALF))
        score(0, slice(HALF, M))
        for r in range(1, PACK):
            score(r, slice(0, M))

        def invert(lo, hi):
            nc.vector.reciprocal(inverse[:, lo:hi], total[:, lo:hi])

        for r in range(PACK):
            if r == last:
                invert(0, 1)
            nc.vector.tensor_reduce(neg_max[r][:], scores[r][:], AXIS_X, MAX, negate=True)
            nc.scalar.activation(expd[r][:], scores[r][:], EXP, bias=neg_max[r][:], accum_out=total[:, r : r + 1])
        quantise_ks(last, PACK, last_bf)
        parts = M // PART

        w_bf = [sb("w_bf%d" % q, [P, PART * PACK], BF16)[:] for q in range(parts)]
        w_codes = [sb("w_codes%d" % q, [P, PART], U32) for q in range(parts)]
        w_scales = [sb("w_scales%d" % q, [P, PART], U8) for q in range(parts)]
        y_rows = [sb("y_rows%d" % h, [P, PACK, HALF], F32) for h in range(2)]
        y_bf = [sb("y_bf%d" % q, [P, PART * PACK], BF16) for q in range(parts)]
        y_codes = sb("y_codes", [P, M], U32)
        y_scales = sb("y_scales", [P, M], U8)
        out_rows = out_0.rearrange("(p t) m -> p t m", t=PACK)
        out_words = out_1.rearrange("z p m t -> p (z m t)").bitcast(I32)

        def weigh(dst, r, src):
            nc.vector.tensor_scalar(dst, src, inverse[:, r : r + 1], fac4[:, r : r + 1], MULT, MULT)

        def every_other(r, odd):
            return expd[r][:].rearrange("s (h e m) -> s h e m", h=2, e=2)[:, :, odd, :]

        def weigh_rows(r, odd):
            weigh(w_rows[odd][:, r, :].rearrange("s (h m) -> s h m", h=2), r, every_other(r, odd))

        def weigh_odd(r):
            dst = w_rows[1][:, r, :].rearrange("s (h m) -> s h m", h=2)
            nc.scalar.activation(dst, every_other(r, 1), COPY, scale=share[:, r : r + 1])

        def weave_w(move, q):
            weave(move, w_bf[q], w_rows[q % 2][:, :, q // 2 * PART : (q // 2 + 1) * PART])

        def quantise_w(q):
            quantise(w_codes[q][:], w_scales[q][:], w_bf[q])

        def product(q, planes, tag):
            sums = psum.tile([P, len(planes), PART], F32, name="sums", tag=tag, bufs=1)
            for t in planes:
                rows = slice(t * P, (t + 1) * P)
                multiply(sums[:, t - planes[0], :], ks_codes[:, rows], ks_scales[:, rows], w_codes[q][:], w_scales[q][:])
            return sums

        def y_part(q):
            return y_rows[q // 2][:, :, q % 2 * PART : (q % 2 + 1) * PART]

        def weave_y(q):
            cut = LAST_SHARE if q == parts - 1 else 0
            weave(nc.vector.tensor_copy, y_bf[q][:, cut * PACK :], y_part(q)[:, :, cut:])
            if cut:
                weave(nc.scalar.copy, y_bf[q][:, : cut * PACK], y_part(q)[:, :, :cut])

        def quantise_y(q):
            cols = slice(q * PART, (q + 1) * PART)
            quantise(y_codes[:, cols], y_scales[:, cols], y_bf[q][:])

        invert(1, 2)
        weigh_rows(0, 0)
        invert(2, last)
        nc.vector.tensor_tensor(share[:], inverse[:, :2], fac4[:, :2], MULT)
        for r in range(2):
            weigh_odd(r)
        weigh_rows(1, 0)
        weigh_rows(2, 0)
        invert(last, PACK)
        for r in range(2, PACK):
            weigh_rows(r, 1)
        nc.vector.tensor_copy(
            w_bf[0].rearrange("s (c i r) -> s c r i", i=4, r=PACK)[:, :, :last, :],
            w_rows[0][:, :last, :PART].rearrange("s r (c i) -> s c r i", i=4),
        )
        weigh(w_bf[0].rearrange("s (m r) -> s m r", r=PACK)[:, :, last], last, expd[last][:, :PART])
        weigh(w_rows[0][:, last, PART:], last, expd[last][:, HALF : HALF + PART])
        weave_w(nc.scalar.copy, 1)
        weave_w(nc.scalar.copy, 3)
        quantise_w(0)
        weave_w(nc.vector.tensor_copy, 2)
        banks = [[product(0, range(2), "spare"), product(0, range(2, PACK), "ksc_rows")]]
        quantise_w(1)
        banks.append([product(1, range(2), "bank0"), product(1, range(2, PACK), "bank1")])

        def fetch(q):
            if len(banks[q]) == 2:
                nc.vector.tensor_copy(y_part(q)[:, :2, :], banks[q][0][:])
                nc.scalar.copy(y_part(q)[:, 2:, :], banks[q][1][:])
            else:
                nc.scalar.copy(y_part(q), banks[q][0][:])
            if q < 2:
                nc.sync.dma_start(out_rows[:, :, q * PART : (q + 1) * PART], y_part(q))

        for q in range(2, parts):
            quantise_w(q)
            if q == 2:
                banks.append([product(q, range(PACK), "bank2")])
                fetch(0)
            else:
                banks.append([product(q, range(2), "bank3"), product(q, range(2, PACK), "spare")])
        for q in range(1, parts):
            fetch(q)
        for h in range(2):
            for step in (weave_y, quantise_y):
                step(2 * h)
                step(2 * h + 1)
            if h == 0:
                nc.sync.dma_start(out_rows[:, :, HALF:], y_rows[1][:])
        nc.sync.dma_start(out_words, y_codes[:].bitcast(I32))
        for quad in range(4):
            queue = nc.sync if quad % 2 else nc.scalar
            queue.dma_start(
                out_2[0, 4 * quad : 4 * quad + 4, :].bitcast(I32), y_scales[32 * quad : 32 * quad + 4, :].bitcast(I32)
            )
